import numpy as np, ml_dtypes
CORES = [16,18,20,22]
N = 4
BF = ml_dtypes.bfloat16
def gentries(a):
    return np.ascontiguousarray(a.reshape(8, 16, -1).transpose(0, 2, 1)).reshape(8, -1)
def gtable(e):
    e = np.asarray(e); return np.ascontiguousarray(e.reshape(8, -1, 16).transpose(0, 2, 1)).reshape(128, -1).astype(np.int32)
E, LEN, NC, RO, DR, DG = 4096, 16, 256, 5, 1, 1
MOD = (4, 4, 4, 4)
KINDS = np.array([1, 1, 2, 15, 16]); WAYS = np.array([0, 1, 2]); ROWS16 = np.arange(16)
def some(rng, kd, rows):
    i = rng.choice(rows, kd.shape); j = (i + rng.integers(1, 16, kd.shape)) & 15; row = np.arange(16).reshape(1, 1, 16, 1)
    return np.where(kd == 1, row == i, np.where(kd == 2, (row == i) | (row == j), (kd == 16) | (row != i))), row == i
def soil(rng, s, x, rate, kinds, ways, rows):
    sh = x.shape[:2] + (1, x.shape[3]); hit = rng.random(sh) < rate; on, first = some(rng, rng.choice(kinds, sh), rows); on = on & hit
    way = rng.choice(ways, sh); dl = rng.integers(1, 4, sh) * (2 * rng.integers(0, 2, sh) - 1); dl = np.where(first, dl, -dl)
    y = x + dl; y = np.where(np.abs(y) > 7, x - dl, y)
    return np.where(on & (way != 1), -s, s), np.where(on & (way != 0), y, x)
def graph(rng):
    A = E // 16; a = np.arange(A); nx = np.zeros((A, 8), np.int64); w = 1
    for i in range(4):
        m = MOD[i]; z = (a // w) % m
        nx[:, 2 * i] = a + ((z + 1) % m - z) * w; nx[:, 2 * i + 1] = a + ((z - 1) % m - z) * w; w *= m
    tau = np.argsort(rng.random((A, 8)), axis=1); inv = np.argsort(tau, axis=1); hi = np.argsort(rng.random((8, E // 8)), axis=1)
    nm = 8 * hi[tau[:, :, None], 2 * a[:, None, None] + np.arange(2)] + tau[:, :, None]
    at = np.zeros(E, np.int64); dr = np.zeros(E, np.int64); at[nm] = a[:, None, None]; dr[nm] = np.arange(8)[None, :, None]
    far = nx[at, dr]; j = np.ascontiguousarray(inv[far].T)
    sq = np.concatenate([nm[at, j, rng.integers(0, 2, (8, E))], nm[nx[at, j], dr, rng.integers(0, 2, (8, E))]])
    h = rng.integers(0, 8, (N, 8, NC, LEN // 2)); d = np.concatenate([h, h ^ 1], axis=3); d = np.take_along_axis(d, np.argsort(rng.random(d.shape), axis=3), 3)
    c = np.zeros(d.shape, np.int64); p = rng.integers(0, A, (N, 8, NC)); t = rng.integers(0, 2, d.shape)
    for i in range(LEN):
        c[..., i] = nm[p, d[..., i], t[..., i]]; p = nx[p, d[..., i]]
    sg = 2 * rng.integers(0, 2, (N, 8, 16, A)) - 1; u = rng.integers(0, 8, (N, 8, 16, A))
    return sg[..., at] * sg[..., far], sg[..., at] * (u[..., at] - u[..., far]), sq, c
def pack(s, x, sq, c):
    return {"v": np.ascontiguousarray((16 * s + x).reshape(N, 128, E)).astype(np.float32).astype(BF), "sq": np.stack([sq] * N).astype(np.int32), "lp": np.stack([gtable(a.reshape(8, -1)) for a in c])}
def skew(rng, shape, w):
    z = (E * rng.random(shape) ** w).astype(np.int64)
    return np.where(rng.random(shape) < 0.5, z, E - 1 - z)
def signs(rng, *shape):
    return 2 * rng.integers(0, 2, shape) - 1
def setup_inputs(rng):
    s, x, sq, c = graph(rng)
    s, x = soil(rng, s, x, rng.choice(np.array([0.03, 0.08, 0.15, 0.22]), (N, 8, 1, 1)), KINDS, WAYS, ROWS16)
    return pack(s, x, sq, c)
def setup_inputs_near(rng):
    s, x, sq, c = graph(rng)
    for b, kinds, ways, rows in ((0, [1], [0], [15]), (1, [2], [1], list(range(16))), (2, [1], [1], [0, 7, 8, 15]), (3, [15, 16], [0, 1, 2], list(range(16)))):
        s[:, b::4], x[:, b::4] = soil(rng, s[:, b::4], x[:, b::4], 0.15, np.array(kinds), np.array(ways), np.array(rows))
    return pack(s, x, sq, c)
def setup_inputs_spread(rng):
    s = np.repeat(signs(rng, N, 8, 16, 1), 5, axis=3); x = np.repeat(rng.integers(-7, 8, (N, 8, 16, 1)), 5, axis=3)
    s[..., 1:3], x[..., 1:3] = soil(rng, s[..., 1:3], x[..., 1:3], 1.0, KINDS, WAYS, ROWS16)
    s[..., 3:] = signs(rng, N, 8, 16, 2); x[..., 3:] = rng.integers(-7, 8, (N, 8, 16, 2))
    who = (5 * rng.random((N, 8, E)) ** rng.choice(np.array([4.0, 8.0, 16.0]), (N, 8, 1))).astype(np.int64)[:, :, None, :]
    w = np.array([1.0, 2.0, 4.0])
    return pack(np.take_along_axis(s, who, 3), np.take_along_axis(x, who, 3), skew(rng, (16, E), rng.choice(w, (16, 1))), skew(rng, (N, 8, NC, LEN), rng.choice(w, (N, 8, 1, 1))))
def setup_inputs_ends(rng):
    M = E - 1; s0 = signs(rng, N, 8, 16, 1); x0 = 7 * s0 * np.where(rng.random(s0.shape) < 0.85, 1, -1)
    kd = rng.choice(np.array([1, 2, 15, 16]), (N, 8, 1, 2)); on, first = some(rng, kd, ROWS16); way = rng.integers(0, 3, kd.shape)
    s = np.concatenate([s0, np.where(on & (way != 2), -s0, s0)], axis=3); x = np.concatenate([x0, np.where(on & (way != 1), -x0, x0)], axis=3)
    who = rng.choice(np.array([0, 1, 2]), (N, 8, E), p=[0.7, 0.15, 0.15]); q = np.arange(N)[:, None]
    who[..., 0] = 0; who[..., M] = np.where((q + np.arange(8)) % 4 == 3, 1 + (q & 1), 0)
    s = np.take_along_axis(s, who[:, :, None, :], 3); x = np.take_along_axis(x, who[:, :, None, :], 3)
    s[:, 7, 15] = 1; x[:, 7, 15] = 7; s[:, 7, 0] = 1; x[:, 7, 0] = -7
    sq = np.where(rng.random((16, E)) < 0.72, M * rng.integers(0, 2, (16, E)), rng.integers(0, E, (16, E)))
    for e, k, f2, e2 in ((0, 0, 0, M), (0, 7, M, M), (M, 7, M, 0), (M, 0, 0, 0)):
        sq[k, e] = f2; sq[8 + k, e] = e2
    c = np.where(rng.random((N, 8, NC, LEN)) < 0.72, M * rng.integers(0, 2, (N, 8, NC, LEN)), rng.integers(0, E, (N, 8, NC, LEN)))
    return pack(s, x, sq, c)
def setup_inputs_corners(rng):
    M = E - 1; e = np.arange(E); reg = ((np.arange(N)[:, None] + np.arange(8) + rng.integers(0, 8)) % 8).reshape(N, 8, 1, 1)
    s = np.repeat(signs(rng, N, 8, 16, 1), E, axis=3); x = np.repeat(rng.integers(-7, 8, (N, 8, 16, 1)), E, axis=3)
    s, x = soil(rng, s, x, np.where(reg == 1, 0.15, 0.0), KINDS, WAYS, ROWS16)
    s, x = soil(rng, s, x, np.where(reg == 3, 0.25, 0.0), np.array([1, 16]), WAYS, ROWS16)
    s = np.where(reg == 2, signs(rng, N, 8, 16, E), s); x = np.where(reg == 2, rng.integers(-7, 8, (N, 8, 16, E)), x)
    row = np.arange(16).reshape(1, 1, 16, 1); own = rng.integers(0, 16, (N, 8, 1, 1)); low = np.minimum(own, 14); odd = (np.arange(N) & 1).reshape(N, 1, 1, 1) == 1
    two = rng.integers(0, 2, (N, 8, 1, E)); three = rng.integers(0, 3, (N, 8, 1, E))
    x = np.where((reg == 4) & (row == own), rng.integers(-3, 4, (N, 8, 1, 1)) + 4 - 8 * two, x)
    m = np.where(odd, rng.integers(1, 8, (N, 8, 1, 1)), 4)
    x = np.where((reg == 5) & (row == low), m * two, x); x = np.where((reg == 5) & (row == low + 1), -two, x); s = np.where((reg == 5) & ((row == low) | (row == low + 1)), 1, s)
    x = np.where((reg == 6) & (row == own), np.where(three > 0, 7, -7), x); s = np.where((reg == 6) & (row == own), np.where(three == 2, -1, 1), s)
    x = np.where((reg == 7) & (row == own), np.where(odd, 6 + two, -6 - two), x); s = np.where((reg == 7) & (row == own), 1, s)
    a = np.stack([e, 0 * e, 0 * e + M, (e + 1) % E, (e - 1) % E])
    sq = np.where(rng.random((16, E)) < 0.4, rng.integers(0, E, (16, E)), a[rng.integers(0, 5, (16, E)), e])
    b = rng.integers(0, E, (N, 8, NC, 1)); i = np.arange(LEN).reshape(1, 1, 1, LEN); z = np.zeros((N, 8, NC, LEN), np.int64)
    c = np.choose(rng.integers(0, 6, (N, 8, NC, 1)), [b + z, M * (i & 1) + z, (b + i) % E, rng.integers(0, E, z.shape), z, z + M])
    return pack(s, x, sq, c)
def setup_inputs_crowd(rng):
    s = np.repeat(signs(rng, N, 8, 16, 1), E, axis=3); x = np.repeat(rng.integers(-7, 8, (N, 8, 16, 1)), E, axis=3)
    s, x = soil(rng, s, x, 0.12, KINDS, WAYS, ROWS16)
    sq = rng.integers(0, E, (16, E)); c = rng.integers(0, E, (N, 8, NC, LEN)); o = int(rng.integers(0, 4))
    for q in range(N):
        for g in range(8):
            m = (q + g + o) % 4; n = rng.integers(0, E, 3)
            if m < 2: c[q, g] = n[0]
            if m == 1: c[q, g, (NC - 1, 0, int(rng.integers(0, NC)))[g % 3], (LEN - 1, 0)[q & 1]] = (int(n[0]) + 1 + int(rng.integers(0, E - 1))) % E
            if m == 2: c[q, g] = n[rng.integers(0, 3, (NC, LEN))]
    return pack(s, x, sq, c)
def check_inputs(d):
    bad = []; a = np.asarray(d["v"]).astype(np.float64)
    if not np.all((np.abs(a) >= 9) & (np.abs(a) <= 23) & (a == np.floor(a))): bad.append("range of v")
    for k in ("sq", "lp"):
        if np.min(d[k]) < 0 or np.max(d[k]) > E - 1: bad.append("range of " + k)
    if not np.all(np.asarray(d["sq"]) == np.asarray(d["sq"])[:1]): bad.append("sq alike on all ranks")
    return bad
def reference(v, sq, lp):
    w = v.astype(np.float32).astype(np.int64).reshape(N, 8, 16, E); tab = sq.astype(np.int64); q = np.arange(N).reshape(N, 1, 1, 1)
    c = np.stack([gentries(a) for a in lp]).astype(np.int64).reshape(N, 8, NC, LEN)
    def pick(names):
        a = np.take_along_axis(w, names.reshape(N, 8, 1, -1), 3); s = np.where(a > 0, 1, -1)
        return s, a - 16 * s
    for rnd in range(RO):
        par = rnd & 1; c = np.roll(c, -par, axis=3); e = c[..., 0::2]; f = c[..., 1::2]; k = f & 7
        f2 = tab[q, k, e]; e2 = tab[q, 8 + k, e]
        se, xe = pick(e); sf, xf = pick(f); sf2, xf2 = pick(f2); se2, xe2 = pick(e2)
        ok = np.all((xe + se * xf == xf2 + sf2 * xe2) & (se * sf == sf2 * se2), axis=2).reshape(e.shape)
        c = np.stack([np.where(ok, f2, e), np.where(ok, e2, f)], axis=4).reshape(N, 8, NC, LEN); c = np.roll(c, par, axis=3)
        c = np.roll(c, DR, axis=0); c[:, :, 1::2] = np.roll(c[:, :, 1::2], DG, axis=1)
    s, x = pick(c); s = s.reshape(N, 8, 16, NC, LEN); x = x.reshape(N, 8, 16, NC, LEN)
    before = np.concatenate([np.ones_like(s[..., :1]), np.multiply.accumulate(s, axis=4)[..., :-1]], axis=4)
    b = np.add.reduce(before * x, axis=4)
    return {"yc": np.stack([gtable(a.reshape(8, -1)) for a in c]).astype(np.float32), "yb": b.reshape(N, 128, NC).astype(np.float32)}

@@ -1,0 +1,350 @@
+from concourse.mybir import AluOpType, ActivationFunctionType
+
+ALU = AluOpType
+ACT = ActivationFunctionType
+E, RO = 4096, 5
+CFG = {
+    "chunks": [32, 32, 32, 32],
+    "sign": "AVAVAVAA",
+    "mq": "VVAVAVAA", "qq": "AVAAVAAV", "fin": "AAAAAVAVAV",
+    "hb": [2, 3, 4, 5], "db": [6],
+    "engines": 16,
+    "g": 1.56, "f": 1.25, "pe": 0.5, "hop": 120.0, "same": 70.0, "send": 900.0, "fly": 2200.0, "eps": 60.0, "beta": 1500.0,
+    "bias": {'vfs': 14650, 'ase': -600, 'vpw': -6300, 'ppw': 14650, 'afw': 1800, 'vs': 6250, 'vfw': 4200, 'ave': 900, 'phpb': 11650,
+             'phnv': 1750, 'vtt': 5000, 'vfu': -9750, 'pxx': 6000, 'vxx': -4100, 'voc': -6350, 'pdl': -10100, 'pzz': 17850,
+             'vns': -9650, 'azz': 7700, 'anv': 8500, 'vpa': 4800, 'vold': -14150, 'vpl': 10150, 'aob': 19900, 'phve': -7100,
+             'vpb': 4550, 'ans': 1600, 'pnx': 14300, 'phpa': -10800, 'amb': 5350},
+}
+MAXC = 6
+OFF = 2048.0
+MAGIC = 12582912.0
+
+
+def _sb(n, dt):
+    return ("sbuf", [128, n], dt)
+
+
+SCRATCH = {
+    "vt": _sb(E, "bfloat16"), "wt": _sb(E, "bfloat16"), "mt": _sb(E, "bfloat16"), "qt": _sb(E, "float32"),
+    "sqi": _sb(512, "int32"), "sqh": _sb(512, "float16"), "le": _sb(256, "int32"), "lf": _sb(256, "int32"),
+    "ki": _sb(16, "int32"), "ci": _sb(16, "int32"), "cf": _sb(16, "float32"), "cg": _sb(16, "float32"),
+    "one": _sb(512, "bfloat16"), "nil": _sb(144, "bfloat16"), "j8": _sb(512, "bfloat16"), "ui": _sb(144, "bfloat16"),
+    "cst": _sb(256, "bfloat16"), "rep": _sb(1024, "bfloat16"), "z1": _sb(144, "bfloat16"), "z2": _sb(512, "bfloat16"),
+    "z3": _sb(144, "bfloat16"), "ni": _sb(128, "bfloat16"), "ph": _sb(384, "bfloat16"), "pn": _sb(384, "bfloat16"),
+    "zh": _sb(288, "bfloat16"), "zn": _sb(288, "bfloat16"),
+    "mb": _sb(2048, "bfloat16"), "ve": _sb(2048, "bfloat16"), "se": _sb(2048, "bfloat16"), "pa": _sb(2048, "bfloat16"),
+    "nv": _sb(2048, "bfloat16"), "ns": _sb(2048, "bfloat16"), "pb": _sb(2048, "bfloat16"), "xx": _sb(2048, "float16"),
+    "old": _sb(512, "float16"), "pw": _sb(256, "float16"), "pl": _sb(256, "uint16"), "zz": _sb(512, "bfloat16"),
+    "tt": _sb(512, "float16"), "fw": _sb(E, "bfloat16"), "fs": _sb(E, "bfloat16"), "fu": _sb(E, "bfloat16"),
+    "oc": _sb(256, "float32"), "ob": _sb(256, "float32"),
+}
+for _t in range(RO + 1):
+    SCRATCH["n%d" % _t] = _sb(256, "uint16")
+for _t in range(RO):
+    SCRATCH["s%d" % _t] = _sb(256, "uint16")
+for _t in range(8):
+    SCRATCH["b%d" % _t] = ("psum", [128, 512], "float32")
+SEMAPHORES = (["cv", "ca", "cp", "cg", "loc"] + ["ld%d" % k for k in range(8)] + ["st%d" % k for k in range(2 * MAXC)]
+              + ["ar%d_%d" % (t, j) for t in range(RO) for j in range(MAXC)])
+COUNTER = {"v": "cv", "a": "ca", "p": "cp", "g": "cg"}
+
+
+def build(g, T, send, cfg):
+    ops, lastw, readers, bank, tag = [], {}, {}, {}, [-1]
+    cyc = 0.83 * cfg["f"]
+    V, S, P = g.vector, g.scalar, g.tensor
+    EQ, MUL, ADD, SUB, AND = ALU.is_equal, ALU.mult, ALU.add, ALU.subtract, ALU.bitwise_and
+
+    def add(q, fn, reads, writes, busy, banks=(), lat=0.0, sem=None, inc=1, after=(), kind=None):
+        i = len(ops); deps = set(); order = set(after)
+        for r in reads:
+            if r in lastw: deps.add(lastw[r])
+        for w in writes:
+            if w in lastw: deps.add(lastw[w])
+            deps.update(readers.get(w, ()))
+        for r in reads: readers.setdefault(r, []).append(i)
+        for w in writes: lastw[w] = i; readers[w] = []
+        for b in banks:
+            cur, prev = bank.get(b, ([], []))
+            if cur and ops[cur[-1]]["q"] == q:
+                deps.update(prev); order.add(cur[-1]); bank[b] = (cur + [i], prev)
+            else:
+                deps.update(cur); bank[b] = ([i], cur)
+        deps.discard(i)
+        ops.append({"q": q, "fn": fn, "deps": deps, "order": order, "busy": busy, "lat": lat, "sem": sem, "inc": inc, "tag": tag[0],
+                    "kind": kind or "%s%s" % (q, "".join(x for x in (list(writes) + [""])[0] if x.isalpha()))})
+        return i
+
+    def vec(fn, reads, writes, n, banks=()):
+        return add("v", fn, reads, writes, cfg.get("ov", 30) + max(64, n) * cyc, banks)
+
+    def sca(fn, reads, writes, n, banks=()):
+        return add("a", fn, reads, writes, cfg.get("oa", 30) + max(64, n) * cyc, banks)
+
+    def gat(q, fn, reads, writes, n):
+        return add(q, fn, reads, writes, (50 if q == "v" else 65) + n * cfg["g"] * cyc)
+
+    def mm(items, reads, b, kind=None):
+        def fn():
+            r = None
+            for o, l, x, st, sp, c in items: r = P.matmul(o, l, x, st, sp)
+            return r
+        return add("p", fn, reads, [], 30 + sum(it[5] for it in items) * cfg["pe"] * cfg["f"], [b], kind="p" + (kind or reads[0][:2]))
+
+    def dma(q, out, in_, reads, writes, sem, lat):
+        e = g.sync if q == "s" else S
+        return add(q, lambda: e.dma_start(out, in_), reads, writes, 60.0, lat=lat * cfg.get("ld", 1.0), sem=sem, inc=16)
+
+    def ts(out, in0, a, b, o0, o1=None):
+        if o1 is None: return lambda: V.tensor_scalar(out, in0, a, None, o0)
+        return lambda: V.tensor_scalar(out, in0, a, b, o0, o1)
+
+    def iota(out, pat, base, cm, key, n, small):
+        if small: fn = lambda: g.iota(out, pat, base, cm, allow_small_or_imprecise_dtypes=True)
+        else: fn = lambda: g.iota(out, pat, base, cm)
+        return add("g", fn, [], [key], 130 + 2 * n * cyc)
+
+    def sel(out, in_, pat, op, fill, base, cm, reads, key, n):
+        return add("g", lambda: g.affine_select(out, in_, pat, op, fill, base, cm), reads, [key], 170 + 2 * n * cyc)
+
+    B = [T["b%d" % k] for k in range(8)]
+    dma("s", T.sqi[:], T.sq[:], [], ["sqi"], "ld0", 2600)
+    dma("a", T.le[0::2, :], T.lp[0::2, :], [], ["le0"], "ld1", 2800)
+    dma("a", T.le[1::2, 0:255], T.lp[0::2, 1:256], [], ["le1"], "ld2", 2900)
+    dma("a", T.lf[0::2, :], T.lp[1::2, :], [], ["lf0"], "ld3", 3000)
+    dma("a", T.lf[1::2, 0:255], T.lp[1::2, 1:256], [], ["lf1"], "ld4", 3100)
+    dma("s", T.vt[:, 0:2048], T.v[:, 0:2048], [], ["v0"], "ld5", 4500)
+    dma("s", T.vt[:, 2048:E], T.v[:, 2048:E], [], ["v1"], "ld6", 6000)
+    VT = ["v0", "v1"]
+    vec(lambda: V.memset(T.one[:], 1.0), [], ["one"], 256)
+    vec(lambda: V.memset(T.nil[:], 0.0), [], ["nil"], 72)
+    iota(T.ki[:, 0:10], [[2, 10]], 0, 1, "ki", 10, False)
+    iota(T.j8[:], [[0, 64], [1, 8]], 0, 0, "j8", 512, True)
+    for u in range(2):
+        sel(T.rep[:, 512 * u:512 * u + 512], T.one[:], [[1, 4], [0, 8], [8, 16]], EQ, 0.0, 4 * u, -1, ["one"], "rep%d" % u, 512)
+    sel(T.z1[:], T.one[:, 0:144], [[-8, 18], [1000, 8]], ALU.is_ge, 0.0, -7000, 1, ["one"], "z1", 144)
+    sel(T.z1[:], T.z1[:], [[8, 18], [0, 8]], ALU.is_ge, 0.0, 7, -1, ["z1"], "z1", 144)
+    for w in range(2):
+        for a in range(2):
+            x = 128 * (2 * w + a)
+            sel(T.z2[:, x:x + 128], T.one[:, 0:128], [[16, 8], [1000, 2], [1, 8]], EQ, 0.0, 8 * w - 1000 * a, -1, ["one"], "z2%d" % (2 * w + a), 128)
+    Z2 = ["z20", "z21", "z22", "z23"]
+    for j in range(4):
+        sel(T.z3[:], T.z3[:] if j else T.nil[:], [[-16, 9], [1000, 4], [-4, 4]], ALU.not_equal, 64.0 ** j, -3000 - j, 1, ["z3" if j else "nil"], "z3", 144)
+    sel(T.ni[:], T.nil[:, 0:128], [[1, 128]], ALU.not_equal, -1.0, 0, -1, ["nil"], "ni", 128)
+    iota(T.ui[:], [[1, 144]], 0, 0, "ui", 144, True)
+    iota(T.cst[:], [[-2048, 2], [0, 128]], 2048, 0, "cst", 256, True)
+    k0 = T.ki[:, 0:1]
+    cf = lambda k: T.cf[:, k:k + 1]
+    cg = lambda k: T.cg[:, k:k + 1]
+    vec(ts(T.ci[:, 0:1], k0, 7, None, AND), ["ki"], ["ci0"], 1)
+    vec(lambda: V.tensor_copy(cf(0), T.ci[:, 0:1]), ["ci0"], ["cf0"], 1)
+    MT = []
+    for k in range(8):
+        x = T.mt[:, 512 * k:512 * k + 512]; MT.append("m%d" % k)
+        if cfg["mq"][k] == "V": vec(ts(x, T.j8[:], cf(0), None, EQ), ["j8", "cf0"], ["m%d" % k], 256)
+        else: sca(lambda x=x: S.activation(x, T.mt[:, 0:512], ACT.Copy), ["m0"], ["m%d" % k], 512)
+    vec(ts(T.ci[:, 3:5], T.ki[:, 0:9:8], 112, None, AND), ["ki"], ["ci3"], 1)
+    vec(ts(T.ci[:, 6:7], k0, 1, None, AND), ["ki"], ["ci6"], 1)
+    vec(ts(T.ci[:, 7:10], T.ki[:, 7:10], 15, None, AND), ["ki"], ["ci7"], 1)
+    vec(ts(T.ci[:, 5:6], k0, 14, None, AND), ["ki"], ["ci5"], 1)
+    vec(lambda: V.tensor_copy(T.cf[:, 3:10], T.ci[:, 3:10]), ["ci3", "ci5", "ci6", "ci7"], ["cf"], 1)
+    vec(ts(cg(5), cf(4), cf(3), cf(6), SUB, MUL), ["cf"], ["cg5"], 1)
+    vec(ts(T.cg[:, 6:9], T.cf[:, 7:10], cf(3), None, ADD), ["cf"], ["cg6"], 1)
+    for d in range(3):
+        vec(ts(T.ph[:, 128 * d:128 * d + 128], T.ui[:, 0:128], cg(5), cg(6 + d), SUB, EQ), ["ui", "cg5", "cg6"], ["ph%d" % d], 64)
+    sca(lambda: S.activation(T.pn[:], T.ph[:], ACT.Copy, scale=-1.0), ["ph0", "ph1", "ph2"], ["pn"], 384)
+    vec(ts(cg(9), cf(5), cf(3), 1.0, ADD, ADD), ["cf"], ["cg9"], 1)
+    vec(ts(cg(10), cg(9), cg(5), None, ADD), ["cg9", "cg5"], ["cg10"], 1)
+    vec(ts(cg(11), cf(6), -1.0, 1.0, MUL, ADD), ["cf"], ["cg11"], 1)
+    for h in range(2):
+        vec(ts(T.zh[:, 144 * h:144 * h + 144], T.ui[:], cg(10), cf(6) if h else cg(11), EQ, MUL), ["ui", "cg10", "cg11", "cf"], ["zh%d" % h], 72)
+    sca(lambda: S.activation(T.zn[:], T.zh[:], ACT.Copy, scale=-1.0), ["zh0", "zh1"], ["zn"], 288)
+    vec(ts(T.old[:], T.one[:], OFF, None, MUL), ["one"], ["top"] + ["old%d" % j for j in range(MAXC)], 256)
+    vec(ts(T.sqh[:], T.sqi[:], -OFF, None, ADD), ["sqi"], ["sqh"], 512)
+    for q in range(8):
+        mm([(B[q][:], T.rep[:, 128 * q:128 * q + 128], T.sqh[:], True, True, 512)], ["sqh", "rep%d" % (q // 4)], q)
+        o = T.qt[:, 512 * q:512 * q + 512]
+        if cfg["qq"][q] == "V": vec(lambda o=o, q=q: V.tensor_copy(o, B[q][:]), [], ["q%d" % q], 512, [q])
+        else: sca(lambda o=o, q=q: S.activation(o, B[q][:], ACT.Copy), [], ["q%d" % q], 512, [q])
+    QT = ["q%d" % q for q in range(8)]
+    for k in range(2):
+        vec(ts(T.wt[:, 2048 * k:2048 * k + 2048], T.vt[:, 2048 * k:2048 * k + 2048], -16.0, None, ADD), ["v%d" % k], ["w%d" % k], 1024)
+    WT = ["w0", "w1"]
+    chunks = cfg["chunks"]; C = len(chunks); offs = [sum(chunks[:j]) for j in range(C)]
+    for j in range(C):
+        n, o = chunks[j], offs[j]
+        vec(lambda n=n, o=o: V.tensor_copy(T.n0[:, 2 * o:2 * o + n], T.le[:, 2 * o:2 * o + 2 * n:2]), ["le0", "le1"], ["n0e%d" % j], n)
+        vec(lambda n=n, o=o: V.tensor_copy(T.n0[:, 2 * o + n:2 * o + 2 * n], T.lf[:, 2 * o:2 * o + 2 * n:2]), ["lf0", "lf1"], ["n0f%d" % j], n)
+    hb, db = cfg["hb"], cfg["db"]
+
+    def sign(side, j, out, in_, r, w, L):
+        if cfg["sign"][(2 * j + side) % len(cfg["sign"])] == "V":
+            vec(ts(out, in_, 1.0, -1.0, ALU.min, ALU.max), [r], [w], L // 2)
+        else:
+            sca(lambda: S.activation(out, in_, ACT.Sign), [r], [w], L)
+
+    def step(t, j):
+        n, o = chunks[j], offs[j]; L = 16 * n; c = max(64, n)
+        N, SB = T["n%d" % t], T["s%d" % t]
+        kE, kF = ("n0e%d" % j, "n0f%d" % j) if t == 0 else ("n%d_%d" % (t, j),) * 2
+        big = lambda b: b[:, 16 * o:16 * o + L]
+        sm = lambda b: b[:, 2 * o:2 * o + 2 * n]
+        half = lambda b, h: b[:, 2 * o + h * n:2 * o + h * n + n]
+        part = lambda x: T.tt[:, 4 * o + x * n:4 * o + x * n + n]
+        Ei, Fi = half(N, 0), half(N, 1)
+        k = lambda s: "%s%d" % (s, j)
+        H = hb[(t * C + j) % len(hb)]; D = db[(t * C + j) % len(db)]
+
+        def hterm(buf, key, first, last):
+            mm([(B[H][:, 0:4 * n], T.z3[:, 12 - 4 * b:140 - 4 * b], buf[:, 16 * o + b:16 * o + L:4], first and b == 0, last and b == 3, max(64, 4 * n))
+                for b in range(4)], [k(key), "z3"], H, "h" + key)
+
+        def relist(dst, base, own):
+            return [(dst[:, base + w * n:base + w * n + n], T.z2[:, 128 * (2 * w + a):128 * (2 * w + a) + 128],
+                     T.pw[:, 2 * o + a:2 * o + 2 * n:2], own and a == 0, own and a == 1, c) for w in range(2) for a in range(2)]
+
+        gat("a", lambda: S.activation(big(T.mb), T.mt[:].indirect(Fi), ACT.Copy), [kF] + MT, [k("mb")], L)
+        gat("v", lambda: V.tensor_tensor(big(T.xx), T.qt[:].indirect(Ei), big(T.mb), MUL), [kE, k("mb")] + QT, [k("xx")], L)
+        mm([(B[0][:, 0:2 * n], T.z1[:, 7 - b:135 - b], T.xx[:, 16 * o + b:16 * o + L:8], b == 0, b == 7, max(64, 2 * n)) for b in range(8)],
+           [k("xx"), "z1"], 0)
+        vec(ts(sm(T.pw), B[0][:, 0:2 * n], -1.0, None, MUL), [], [k("pw")], 2 * n, [0])
+        mm(relist(B[1], 0, True), [k("pw")] + Z2, 1)
+        vec(ts(sm(T.pl), B[1][:, 0:2 * n], -1.0, OFF, MUL, ADD), [], [k("pl")], 2 * n, [1])
+        gat("a", lambda: S.activation(big(T.ve), T.vt[:].indirect(Ei), ACT.Copy), [kE] + VT, [k("ve")], L)
+        sign(0, j, big(T.se), big(T.ve), k("ve"), k("se"), L)
+        gat("v", lambda: V.tensor_tensor(big(T.pa), T.wt[:].indirect(Fi), big(T.se), MUL), [kF, k("se")] + WT, [k("pa")], L)
+        vec(ts(T.old[:, 4 * o:4 * o + 2 * n], sm(N), -OFF, None, ADD), [kE, kF], [k("old")], n)
+        gat("a", lambda: S.activation(big(T.nv), T.vt[:].indirect(half(T.pl, 0)), ACT.Copy, scale=-1.0), [k("pl")] + VT, [k("nv")], L)
+        sign(1, j, big(T.ns), big(T.nv), k("nv"), k("ns"), L)
+        gat("v", lambda: V.tensor_tensor(big(T.pb), T.wt[:].indirect(half(T.pl, 1)), big(T.ns), MUL), [k("pl"), k("ns")] + WT, [k("pb")], L)
+        hterm(T.ve, "ve", True, False); hterm(T.pa, "pa", False, False)
+        hterm(T.nv, "nv", False, False); hterm(T.pb, "pb", False, True)
+        sca(lambda: S.activation(T.zz[:, 4 * o:4 * o + 4 * n], B[H][:, 0:4 * n], ACT.Abs, scale=2 * OFF), [], [k("zz")], 4 * n, [H])
+        mm([(B[D][:, 0:4 * n], T.ni[:], T.cst[:, 128 - 2 * n:128 + 2 * n], True, False, max(64, 4 * n))] + relist(B[D], 2 * n, False),
+           [k("pw"), "ni", "cst"] + Z2, D, "dl")
+        mm([(B[D][:, w * n:w * n + n], T.z3[:, 12 - 4 * a:140 - 4 * a], T.zz[:, 4 * o + a:4 * o + 4 * n:4], False, w == 3 and a == 3, c)
+            for w in range(4) for a in range(4)], [k("zz"), "z3"], D)
+        vec(lambda: V.tensor_tensor(T.tt[:, 4 * o:4 * o + 4 * n], B[D][:, 0:4 * n], T.old[:, 4 * o:4 * o + 4 * n], ALU.min),
+            [k("old"), "top"], [k("tt")], 4 * n, [D])
+        if t < RO - 1:
+            it, rd = [], ["pn"]
+            for w, d in ((0, 1 if t % 2 == 0 else 2), (1, 0 if t % 2 == 0 else 1)):
+                out = B[7][:, w * n:w * n + n]
+                it += [(out, T.ph[:, 128 * d:128 * d + 128], part(1 - w), True, False, c),
+                       (out, T.pn[:, 128 * d:128 * d + 128], part(3 - w), False, True, c)]
+                rd.append("ph%d" % d)
+        else:
+            it, rd = [], ["zh0", "zh1", "zn"]
+            for h in range(2):
+                for x in range(4):
+                    y = 144 * h + 1 - x % 2
+                    it.append((B[7][:, h:2 * n:2], (T.zh if x < 2 else T.zn)[:, y:y + 128], part(x), x == 0, x == 3, c))
+        mm(it, rd + [k("tt")], 7, "nx")
+        vec(ts(sm(SB), B[7][:, 0:2 * n], 2 * OFF, None, ADD), [], ["s%d_%d" % (t, j)], 2 * n, [7])
+        i = add("g", lambda: send(sm(T["n%d" % (t + 1)]), sm(SB), T.sem["ar%d_%d" % (t, j)]), ["s%d_%d" % (t, j)], [], cfg["send"], sem="loc", inc=0)
+        add(None, None, [], ["n%d_%d" % (t + 1, j)], 0.0, lat=cfg["fly"], sem="ar%d_%d" % (t, j), inc=cfg["engines"], after=[i])
+
+    def last(j):
+        n, o = chunks[j], offs[j]; L = 32 * n; a = 32 * o
+        N = T["n%d" % RO]; kN = "n%d_%d" % (RO, j)
+        k = lambda s: "%s%d" % (s, j)
+        sm = lambda b: b[:, 2 * o:2 * o + 2 * n]
+        rev = lambda b: b[:, a + L - 1:a - 1:-1] if a else b[:, L - 1::-1]
+        end = lambda b: b[:, a + 15:a + L:16]
+        for u in range(2):
+            x = a + u * 16 * n
+            out, win = T.fw[:, x:x + 16 * n], T.vt[:].indirect(N[:, 2 * o + u * n:2 * o + u * n + n])
+            if cfg["fin"][2 * j + u] == "A":
+                gat("a", lambda out=out, win=win: S.activation(out, win, ACT.Identity, bias=-1.0, scale=0.0625), [kN] + VT, [k("fw%d_" % u)], L // 2)
+            else:
+                gat("v", ts(out, win, 0.0625, -1.0, MUL, ADD), [kN] + VT, [k("fw%d_" % u)], L // 2)
+            vec(ts(T.fs[:, x:x + 16 * n], out, MAGIC, MAGIC - 1.0, ADD, SUB), [k("fw%d_" % u)], [k("fs%d_" % u)], L // 4)
+        fw, fs = [k("fw0_"), k("fw1_")], [k("fs0_"), k("fs1_")]
+        vec(lambda: V.tensor_tensor(end(T.fw), end(T.fw), end(T.fs), SUB), fs + fw, fw, 4 * n)
+        vec(lambda: V.memset(end(T.fs), 0.0), [], fs, 2 * n)
+        vec(lambda: V.tensor_tensor_scan(rev(T.fu), rev(T.fs), rev(T.fw), 0.0, MUL, ADD), fs + fw, [k("fu")], L // 2)
+        vec(lambda: V.tensor_copy(sm(T.oc), sm(N)), [kN], [k("oc")], 2 * n)
+        sca(lambda: S.activation(sm(T.ob), T.fu[:, a:a + L:16], ACT.Identity, bias=16.0, scale=16.0), [k("fu")], [k("ob")], 2 * n)
+        dma("s", sm(T.yc), sm(T.oc), [k("oc")], [], "st%d" % (2 * j), 2000)
+        dma("s", sm(T.yb), sm(T.ob), [k("ob")], [], "st%d" % (2 * j + 1), 2000)
+
+    for t in range(RO):
+        for j in range(C): tag[0] = t * C + j; step(t, j)
+    for j in range(C): tag[0] = RO * C + j; last(j)
+    return ops
+
+
+def arrange(ops, cfg):
+    n = len(ops); pre = [sorted(o["deps"] | o["order"]) for o in ops]; post = [[] for _ in ops]
+    for i in range(n):
+        for d in pre[i]: post[d].append(i)
+    rank = [0.0] * n
+    for i in range(n - 1, -1, -1):
+        rank[i] = ops[i]["busy"] + ops[i]["lat"] + max([rank[s] + cfg["hop"] for s in post[i]] + [0.0])
+    for i in range(n):
+        rank[i] += cfg["bias"].get(ops[i]["kind"], 0.0) - cfg["beta"] * max(ops[i]["tag"], 0)
+    left = [len(p) for p in pre]; done = [0.0] * n; free = {}; est = {}; seq = []
+
+    def earliest(i):
+        e = 0.0
+        for d in ops[i]["deps"]: e = max(e, done[d] + (cfg["same"] if ops[d]["q"] == ops[i]["q"] else cfg["hop"]))
+        if ops[i]["q"] is None:
+            for d in ops[i]["order"]: e = max(e, done[d])
+        return e
+    for i in range(n):
+        if not left[i]: est[i] = 0.0
+    while est:
+        st = {i: max(e, free.get(ops[i]["q"], 0.0)) if ops[i]["q"] else e for i, e in est.items()}
+        f = min(st, key=lambda i: (st[i], -rank[i])); q = ops[f]["q"]
+        i = max((x for x in st if ops[x]["q"] == q and st[x] <= st[f] + cfg["eps"]), key=lambda x: (rank[x], -x))
+        if q: free[q] = st[i] + ops[i]["busy"]
+        done[i] = st[i] + ops[i]["busy"] + ops[i]["lat"]; seq.append(i); del est[i]
+        for s in post[i]:
+            left[s] -= 1
+            if not left[s]: est[s] = earliest(s)
+    return seq, max(done)
+
+
+KEPT = {}
+
+
+def rank_program(g, core, T, topo):
+    rank = T.rank_of(core)
+    if rank is None:
+        return
+    cfg = CFG
+    dst = T.cores[(rank + 1) % len(T.cores)]
+    rid, pid = topo.addr(dst)[:2]
+    eng = topo.engines(core, dst); eng = eng[::len(eng) // cfg["engines"]]
+    mask = sum(1 << e for e in eng)
+    send = lambda out, in_, sem: g.remote_dma(out, in_, sem, T.sem.loc, pid, rid, mask)
+    ops = build(g, T, send, cfg)
+    if "seq" not in KEPT: KEPT["seq"] = arrange(ops, cfg)[0]
+    queue = {"v": g.vector, "a": g.scalar, "p": g.tensor, "g": g, "s": g.sync}
+    known = {q: {} for q in queue}; total = {}; mark = {}; carry = {}
+    for i in KEPT["seq"]:
+        o = ops[i]; q = o["q"]
+        if q is None:
+            mark[i] = (o["sem"], o["inc"]); carry[i] = {}; total[o["sem"]] = o["inc"]
+            continue
+        need = {}
+        for d in o["deps"]:
+            s, val = mark[d]
+            if val > need.get(s, (0, 0))[0]: need[s] = (val, d)
+        for s, (val, d) in sorted(need.items(), key=lambda x: -x[1][1]):
+            if known[q].get(s, 0) >= val: continue
+            queue[q].wait_ge(T.sem[s], val)
+            known[q][s] = val
+            for s2, v2 in carry[d].items():
+                if v2 > known[q].get(s2, 0): known[q][s2] = v2
+        r = o["fn"]()
+        if o["sem"] == "loc":
+            total["loc"] = total.get("loc", 0) + len(eng)
+            continue
+        s = o["sem"] or COUNTER[q]
+        r.then_inc(T.sem[s], o["inc"])
+        total[s] = total.get(s, 0) + o["inc"]; mark[i] = (s, total[s]); carry[i] = dict(known[q])
+    for s, val in total.items():
+        if s == "loc": g.wait_ge(T.sem.loc, val)
+        elif all(known[q].get(s, 0) < val for q in queue): g.sync.wait_ge(T.sem[s], val)

@@ -4,20 +4,30 @@ ALU = AluOpType
 ACT = ActivationFunctionType
 E, RO = 4096, 5
 CFG = {
-    "chunks": [32, 32, 32, 32],
-    "sign": "AVAVAVAA",
-    "mq": "VVAVAVAA", "qq": "AVAAVAAV", "fin": "AAAAAVAVAV",
-    "hb": [2, 3, 4, 5], "db": [6],
+    "chunks": [28, 28, 24, 24, 24],
+    "lin": {"rr": "V", "pl": "A", "old": "A", "sb": "V", "fl": "A", "cc": "V"},
+    "gq": "AVAAVVAV", "wq": "AAAAAAVA", "fin": "AAAAAAAVAAVA",
+    "xb": [0], "rb": [1], "hb": [2, 3], "qb": [4, 5], "db": [6], "yb": [7],
     "engines": 16,
-    "g": 1.56, "f": 1.25, "pe": 0.5, "hop": 120.0, "same": 70.0, "send": 900.0, "fly": 2200.0, "eps": 60.0, "beta": 1500.0,
-    "bias": {'vfs': 14650, 'ase': -600, 'vpw': -6300, 'ppw': 14650, 'afw': 1800, 'vs': 6250, 'vfw': 4200, 'ave': 900, 'phpb': 11650,
-             'phnv': 1750, 'vtt': 5000, 'vfu': -9750, 'pxx': 6000, 'vxx': -4100, 'voc': -6350, 'pdl': -10100, 'pzz': 17850,
-             'vns': -9650, 'azz': 7700, 'anv': 8500, 'vpa': 4800, 'vold': -14150, 'vpl': 10150, 'aob': 19900, 'phve': -7100,
-             'vpb': 4550, 'ans': 1600, 'pnx': 14300, 'phpa': -10800, 'amb': 5350},
+    "mq": [3600, 4400, -100, 3900, 5700, 3900, 1900, 4900], "tw": [2000, 0, 3600, 5000, 8500, 8500, 8800, 8800],
+    "late": [4500, 1000, 9000, 10000, 14000], "start": 7800, "period": 2300,
+    "slots": {'ge': -300, 'xx': 1550, 'mx': 2460, 'rr': 3270, 'zq': 3280, 'ml': 3520, 'pl': 4230, 'gn': 4240, 'pb': 5250, 'mb': 5510, 'fl': 6320, 'mf': 6330, 'zc': 7040, 'mc': 7650, 'tt': 8110, 'mn': 8520, 's': 9160, 'send': 11370, 'n': 11780, 'pa': 3400, 'ma': 4500, 'old': 5000, 'mr': 4510, 'ms': 5520, 'fw': -3800, 'fs': 3500, 'fe': 3510, 'fz': 4520, 'fu': 4530, 'oc': 1800, 'ob': 5040, 'out': 5550},
+    "lat": {"p": 100.0, "a": 80.0}, "g": 1.56, "f": 1.05, "pe": 0.42, "hop": 130.0, "same": 40.0, "send": 400.0, "fly": 1400.0,
+    "ov": 10, "oa": 50,
 }
+CFG.update({'chunks': [28, 28, 24, 24, 24], 'lin': {'rr': 'A', 'pl': 'A', 'old': 'A', 'sb': 'V', 'fl': 'A', 'cc': 'A'}, 'gq': 'VVAAVVAV', 'wq': 'AAAAVVAA', 'fin': 'AVVAAAAAAAAA', 'mq': [4100, 1400, -1400, 4900, 5700, 1900, 1000, -2300], 'tw': [3900, 1700, 7500, 1600, 7100, 8700, 3300, 4700], 'late': [6200, 2000, 7000, 12500, 16400], 'start': 5100, 'period': 2250, 'slots': {'ge': 1000, 'xx': 2310, 'mx': 3720, 'rr': 3930, 'zq': 4040, 'ml': 5090, 'pl': 5600, 'gn': 5710, 'pb': 6220, 'mb': 6820, 'fl': 7830, 'mf': 8130, 'zc': 8240, 'mc': 8650, 'tt': 8960, 'mn': 9820, 's': 9830, 'send': 13240, 'n': 13550, 'pa': 5200, 'ma': 6810, 'old': 7140, 'mr': 6810, 'ms': 8120, 'fw': -2400, 'fs': 4600, 'fe': 6210, 'fz': 6220, 'fu': 6230, 'oc': -9600, 'ob': 11640, 'out': 12850}})
+CFG["split"] = ["ge", "xx", "gn", "pb"]; CFG["scan"] = []
+CFG.update({"sg": [3300, 3350, 4000, 4050, 4700, 4750, 5400, 5450], "tg": [4000, 4300, 4700, 5000, 5400, 5700, 6100, 6200], "oq": "AAAVVVAAAAAA"})
+CFG.update({'chunks': [28, 28, 24, 24, 24], 'lin': {'rr': 'V', 'pl': 'A', 'old': 'A', 'sb': 'A', 'fl': 'A', 'cc': 'V'}, 'gq': 'AAAAVVAV', 'wq': 'VAAAAAVA', 'fin': 'VAAAAAAVAVAA', 'mq': [1800, 2700, -2000, 3500, 6000, -1300, -1100, 4900], 'tw': [5300, 0, 1700, 4700, 7900, 9600, 7700, 9800], 'late': [6000, 1000, 4500, 9200, 16600], 'start': 8100, 'period': 2300, 'slots': {'geh': 100.0, 'gei': 800.0, 'xxh': 110.0, 'xxi': 810.0, 'mx': 1720.0, 'rr': 1930.0, 'zq': 2240.0, 'ml': 2950.0, 'pl': 3410.0, 'gnh': 4140.0, 'gni': 4540.0, 'pbh': 4150.0, 'pbi': 4550.0, 'mb': 5640.0, 'fl': 5850.0, 'ms': 5730.0, 'mf': 6500.0, 'zc': 6610.0, 'mc': 7420.0, 'tt': 7690.0, 'mn': 8200.0, 's': 8810.0, 'send': 8920.0, 'n': 10830.0, 'pah': 810.0, 'pai': -990.0, 'ma': 2100.0, 'mr': 5720.0, 'old': 7180.0, 'fw': 900.0, 'fs': 1110.0, 'fe': 1720.0, 'fz': 2260.0, 'fu': 3070.0, 'oc': 7450.0, 'ob': 3620.0, 'out': 17530.0}})
+CFG.update({'chunks': [28, 28, 24, 24, 24], 'split': ['ge', 'xx', 'gn', 'pb', 'pa'], 'scan': ['pai'], 'sg': [2600, 3050, 4000, 4050, 4300, 4050, 4800, 5450], 'tg': [1700, 3350, 6500, 1250, 5500, 3550, 5700, 6550], 'oq': 'VAAAVAAVVAVA', 'lin': {'rr': 'V', 'pl': 'A', 'old': 'A', 'sb': 'V', 'fl': 'A', 'cc': 'V'}, 'gq': 'VAVAVAVA', 'wq': 'AAAAAVAA', 'fin': 'AVAAAAAAVAVA', 'mq': [8200, 2900, -3900, 4000, 3900, 6300, -300, 4500], 'tw': [500, 4500, 2200, 3600, 6100, 9100, 5500, 10300], 'late': [6300, 3800, 4800, 11000, 17900, 1000], 'start': 11100, 'period': 2300, 'slots': {'geh': -2500, 'gei': -2800, 'xxh': -490, 'xxi': -510, 'mx': 1200, 'rr': 1310, 'zq': 1620, 'ml': 2130, 'pl': 3560, 'gnh': 3570, 'gni': 3670, 'pbh': 3580, 'pbi': 4080, 'mb': 5070, 'fl': 5880, 'ms': 5270, 'mf': 5990, 'zc': 6390, 'mc': 7280, 'tt': 7290, 'mn': 8200, 's': 8510, 'send': 9420, 'n': 11630, 'gwh': 20, 'gwi': 640, 'pah': 710, 'pai': 2550, 'ma': 3960, 'mr': 3760, 'old': 6550, 'fw': -3600, 'fs': 2310, 'fe': 2320, 'fz': 2330, 'fu': 2740, 'oc': 4150, 'ob': 5020, 'out': 5430}})
 MAXC = 6
 OFF = 2048.0
 MAGIC = 12582912.0
+K = 1984.0
+M = 2 * K
+W = 61.0
+UP = 2.0 ** 20
+FR = 8192.0
 
 
 def _sb(n, dt):
@@ -25,35 +35,37 @@ def _sb(n, dt):
 
 
 SCRATCH = {
-    "vt": _sb(E, "bfloat16"), "wt": _sb(E, "bfloat16"), "mt": _sb(E, "bfloat16"), "qt": _sb(E, "float32"),
+    "vt": _sb(E, "bfloat16"), "sg": _sb(E, "bfloat16"), "mt": _sb(E, "bfloat16"), "tg": _sb(E, "float32"), "tw": _sb(E, "float32"),
     "sqi": _sb(512, "int32"), "sqh": _sb(512, "float16"), "le": _sb(256, "int32"), "lf": _sb(256, "int32"),
     "ki": _sb(16, "int32"), "ci": _sb(16, "int32"), "cf": _sb(16, "float32"), "cg": _sb(16, "float32"),
-    "one": _sb(512, "bfloat16"), "nil": _sb(144, "bfloat16"), "j8": _sb(512, "bfloat16"), "ui": _sb(144, "bfloat16"),
-    "cst": _sb(256, "bfloat16"), "rep": _sb(1024, "bfloat16"), "z1": _sb(144, "bfloat16"), "z2": _sb(512, "bfloat16"),
-    "z3": _sb(144, "bfloat16"), "ni": _sb(128, "bfloat16"), "ph": _sb(384, "bfloat16"), "pn": _sb(384, "bfloat16"),
-    "zh": _sb(288, "bfloat16"), "zn": _sb(288, "bfloat16"),
-    "mb": _sb(2048, "bfloat16"), "ve": _sb(2048, "bfloat16"), "se": _sb(2048, "bfloat16"), "pa": _sb(2048, "bfloat16"),
-    "nv": _sb(2048, "bfloat16"), "ns": _sb(2048, "bfloat16"), "pb": _sb(2048, "bfloat16"), "xx": _sb(2048, "float16"),
-    "old": _sb(512, "float16"), "pw": _sb(256, "float16"), "pl": _sb(256, "uint16"), "zz": _sb(512, "bfloat16"),
+    "one": _sb(64, "bfloat16"), "pm": _sb(512, "bfloat16"), "tiny": _sb(512, "bfloat16"), "nil": _sb(128, "bfloat16"), "j8": _sb(256, "bfloat16"),
+    "ui": _sb(144, "bfloat16"), "onef": _sb(16, "float32"), "wx": _sb(16, "float32"), "wb": _sb(72, "bfloat16"),
+    "wp": _sb(72, "bfloat16"), "wn": _sb(72, "bfloat16"), "rep": _sb(1024, "bfloat16"), "idn": _sb(128, "bfloat16"),
+    "ik": _sb(128, "bfloat16"), "im": _sb(128, "bfloat16"),
+    "ri": _sb(1536, "bfloat16"), "ph": _sb(384, "bfloat16"), "zh": _sb(288, "bfloat16"),
+    "ge": _sb(2048, "float32"), "gw": _sb(2048, "float32"), "gn": _sb(2048, "float32"), "xx": _sb(2048, "float32"), "pa": _sb(2048, "float16"), "pb": _sb(2048, "float16"),
+    "rr": _sb(64 * MAXC, "float16"), "fl": _sb(256 * MAXC, "bfloat16"),
+    "zq": ("sbuf", [128, 68 * MAXC, 4], "float16"), "zc": ("sbuf", [128, 36 * MAXC, 4], "bfloat16"),
+    "old": _sb(512, "float16"),
     "tt": _sb(512, "float16"), "fw": _sb(E, "bfloat16"), "fs": _sb(E, "bfloat16"), "fu": _sb(E, "bfloat16"),
     "oc": _sb(256, "float32"), "ob": _sb(256, "float32"),
 }
 for _t in range(RO + 1):
-    SCRATCH["n%d" % _t] = _sb(256, "uint16")
+    SCRATCH["n%d" % _t] = _sb(512, "uint16")
 for _t in range(RO):
     SCRATCH["s%d" % _t] = _sb(256, "uint16")
 for _t in range(8):
     SCRATCH["b%d" % _t] = ("psum", [128, 512], "float32")
-SEMAPHORES = (["cv", "ca", "cp", "cg", "loc"] + ["ld%d" % k for k in range(8)] + ["st%d" % k for k in range(2 * MAXC)]
+SEMAPHORES = (["cv", "ca", "cp", "cg", "loc"] + ["ld%d" % k for k in range(10)] + ["st%d" % k for k in range(2 * MAXC)]
               + ["ar%d_%d" % (t, j) for t in range(RO) for j in range(MAXC)])
 COUNTER = {"v": "cv", "a": "ca", "p": "cp", "g": "cg"}
 
 
 def build(g, T, send, cfg):
-    ops, lastw, readers, bank, tag = [], {}, {}, {}, [-1]
+    ops, lastw, readers, bank, tag, slot = [], {}, {}, {}, [-1], [0]
     cyc = 0.83 * cfg["f"]
     V, S, P = g.vector, g.scalar, g.tensor
-    EQ, MUL, ADD, SUB, AND = ALU.is_equal, ALU.mult, ALU.add, ALU.subtract, ALU.bitwise_and
+    EQ, GE, MUL, ADD, SUB, AND = ALU.is_equal, ALU.is_ge, ALU.mult, ALU.add, ALU.subtract, ALU.bitwise_and
 
     def add(q, fn, reads, writes, busy, banks=(), lat=0.0, sem=None, inc=1, after=(), kind=None):
         i = len(ops); deps = set(); order = set(after)
@@ -71,25 +83,26 @@ def build(g, T, send, cfg):
             else:
                 deps.update(cur); bank[b] = ([i], cur)
         deps.discard(i)
-        ops.append({"q": q, "fn": fn, "deps": deps, "order": order, "busy": busy, "lat": lat, "sem": sem, "inc": inc, "tag": tag[0],
-                    "kind": kind or "%s%s" % (q, "".join(x for x in (list(writes) + [""])[0] if x.isalpha()))})
+        if sem is None: lat += cfg["lat"].get(q, 0.0)
+        ops.append({"q": q, "fn": fn, "deps": deps, "order": order, "busy": busy, "lat": lat, "sem": sem, "inc": inc, "tag": tag[0], "slot": slot[0],
+                    "kind": kind or "".join(x for x in (list(writes) + ["out"])[0] if x.isalpha())})
         return i
 
     def vec(fn, reads, writes, n, banks=()):
-        return add("v", fn, reads, writes, cfg.get("ov", 30) + max(64, n) * cyc, banks)
+        return add("v", fn, reads, writes, cfg["ov"] + max(64, n) * cyc, banks)
 
     def sca(fn, reads, writes, n, banks=()):
-        return add("a", fn, reads, writes, cfg.get("oa", 30) + max(64, n) * cyc, banks)
+        return add("a", fn, reads, writes, cfg["oa"] + max(64, n) * cyc, banks)
 
     def gat(q, fn, reads, writes, n):
         return add(q, fn, reads, writes, (50 if q == "v" else 65) + n * cfg["g"] * cyc)
 
-    def mm(items, reads, b, kind=None):
+    def mm(items, reads, b, kind):
         def fn():
             r = None
             for o, l, x, st, sp, c in items: r = P.matmul(o, l, x, st, sp)
             return r
-        return add("p", fn, reads, [], 30 + sum(it[5] for it in items) * cfg["pe"] * cfg["f"], [b], kind="p" + (kind or reads[0][:2]))
+        return add("p", fn, reads, [], 30 + sum(it[5] for it in items) * cfg["pe"] * cfg["f"], [b], kind=kind)
 
     def dma(q, out, in_, reads, writes, sem, lat):
         e = g.sync if q == "s" else S
@@ -98,6 +111,10 @@ def build(g, T, send, cfg):
     def ts(out, in0, a, b, o0, o1=None):
         if o1 is None: return lambda: V.tensor_scalar(out, in0, a, None, o0)
         return lambda: V.tensor_scalar(out, in0, a, b, o0, o1)
+
+    def lin(e, out, in_, scale, bias, reads, writes, n, banks=(), narrow=False):
+        if e == "V": return vec(ts(out, in_, scale, bias, MUL, ADD), reads, writes, n // 2 if narrow else n, banks)
+        return sca(lambda: S.activation(out, in_, ACT.Identity, bias=bias, scale=scale), reads, writes, n, banks)
 
     def iota(out, pat, base, cm, key, n, small):
         if small: fn = lambda: g.iota(out, pat, base, cm, allow_small_or_imprecise_dtypes=True)
@@ -108,141 +125,163 @@ def build(g, T, send, cfg):
         return add("g", lambda: g.affine_select(out, in_, pat, op, fill, base, cm), reads, [key], 170 + 2 * n * cyc)
 
     B = [T["b%d" % k] for k in range(8)]
+    chunks = cfg["chunks"]; C = len(chunks); offs = [sum(chunks[:j]) for j in range(C)]
     dma("s", T.sqi[:], T.sq[:], [], ["sqi"], "ld0", 2600)
-    dma("a", T.le[0::2, :], T.lp[0::2, :], [], ["le0"], "ld1", 2800)
-    dma("a", T.le[1::2, 0:255], T.lp[0::2, 1:256], [], ["le1"], "ld2", 2900)
-    dma("a", T.lf[0::2, :], T.lp[1::2, :], [], ["lf0"], "ld3", 3000)
-    dma("a", T.lf[1::2, 0:255], T.lp[1::2, 1:256], [], ["lf1"], "ld4", 3100)
-    dma("s", T.vt[:, 0:2048], T.v[:, 0:2048], [], ["v0"], "ld5", 4500)
-    dma("s", T.vt[:, 2048:E], T.v[:, 2048:E], [], ["v1"], "ld6", 6000)
-    VT = ["v0", "v1"]
-    vec(lambda: V.memset(T.one[:], 1.0), [], ["one"], 256)
-    vec(lambda: V.memset(T.nil[:], 0.0), [], ["nil"], 72)
-    iota(T.ki[:, 0:10], [[2, 10]], 0, 1, "ki", 10, False)
-    iota(T.j8[:], [[0, 64], [1, 8]], 0, 0, "j8", 512, True)
-    for u in range(2):
-        sel(T.rep[:, 512 * u:512 * u + 512], T.one[:], [[1, 4], [0, 8], [8, 16]], EQ, 0.0, 4 * u, -1, ["one"], "rep%d" % u, 512)
-    sel(T.z1[:], T.one[:, 0:144], [[-8, 18], [1000, 8]], ALU.is_ge, 0.0, -7000, 1, ["one"], "z1", 144)
-    sel(T.z1[:], T.z1[:], [[8, 18], [0, 8]], ALU.is_ge, 0.0, 7, -1, ["z1"], "z1", 144)
-    for w in range(2):
-        for a in range(2):
-            x = 128 * (2 * w + a)
-            sel(T.z2[:, x:x + 128], T.one[:, 0:128], [[16, 8], [1000, 2], [1, 8]], EQ, 0.0, 8 * w - 1000 * a, -1, ["one"], "z2%d" % (2 * w + a), 128)
-    Z2 = ["z20", "z21", "z22", "z23"]
-    for j in range(4):
-        sel(T.z3[:], T.z3[:] if j else T.nil[:], [[-16, 9], [1000, 4], [-4, 4]], ALU.not_equal, 64.0 ** j, -3000 - j, 1, ["z3" if j else "nil"], "z3", 144)
-    sel(T.ni[:], T.nil[:, 0:128], [[1, 128]], ALU.not_equal, -1.0, 0, -1, ["nil"], "ni", 128)
-    iota(T.ui[:], [[1, 144]], 0, 0, "ui", 144, True)
-    iota(T.cst[:], [[-2048, 2], [0, 128]], 2048, 0, "cst", 256, True)
+    for k in range(4):
+        dma("as"[k % 2], T.vt[:, 1024 * k:1024 * k + 1024], T.v[:, 1024 * k:1024 * k + 1024], [], ["v%d" % k], "ld%d" % (5 + k), 3300 + 700 * k)
+    VT = ["v%d" % k for k in range(4)]
+    dma("a", T.le[0::2, :], T.lp[0::2, :], [], ["le0"], "ld1", 5600)
+    dma("s", T.le[1::2, 0:255], T.lp[0::2, 1:256], [], ["le1"], "ld2", 5700)
+    dma("a", T.lf[0::2, :], T.lp[1::2, :], [], ["lf0"], "ld3", 5800)
+    dma("s", T.lf[1::2, 0:255], T.lp[1::2, 1:256], [], ["lf1"], "ld4", 5900)
     k0 = T.ki[:, 0:1]
     cf = lambda k: T.cf[:, k:k + 1]
     cg = lambda k: T.cg[:, k:k + 1]
+    iota(T.ki[:, 0:10], [[2, 10]], 0, 1, "ki", 10, False)
+    iota(T.j8[:], [[0, 32], [1, 8]], 0, 0, "j8", 256, True)
+    vec(lambda: V.memset(T.tiny[:], 1.0 / FR), [], ["tiny"], 256)
+    vec(lambda: V.memset(T.nil[:], 0.0), [], ["nil"], 64)
     vec(ts(T.ci[:, 0:1], k0, 7, None, AND), ["ki"], ["ci0"], 1)
+    vec(lambda: V.memset(T.one[:], 1.0), [], ["one"], 32)
+    y = 2 * OFF if cfg["lin"]["cc"] == "V" else OFF
+    for u in range(2): vec(lambda u=u, y=y: V.memset(T.pm[:, 256 * u:256 * u + 256], y - 2 * u * y), [], ["pm%d" % u], 128)
     vec(lambda: V.tensor_copy(cf(0), T.ci[:, 0:1]), ["ci0"], ["cf0"], 1)
-    MT = []
-    for k in range(8):
-        x = T.mt[:, 512 * k:512 * k + 512]; MT.append("m%d" % k)
-        if cfg["mq"][k] == "V": vec(ts(x, T.j8[:], cf(0), None, EQ), ["j8", "cf0"], ["m%d" % k], 256)
-        else: sca(lambda x=x: S.activation(x, T.mt[:, 0:512], ACT.Copy), ["m0"], ["m%d" % k], 512)
+    vec(lambda: V.memset(T.onef[:], 1.0), [], ["onef"], 16)
+    for u in range(2):
+        sel(T.rep[:, 512 * u:512 * u + 512], T.tiny[:], [[1, 4], [0, 8], [8, 16]], EQ, 0.0, 4 * u, -1, ["tiny"], "rep%d" % u, 512)
+    for name, x in (("ik", K - 16), ("idn", 1.0)):
+        sel(T[name][:], T.nil[:], [[1, 128]], ALU.not_equal, x, 0, -1, ["nil"], name, 128)
+    vec(ts(T.mt[:, 0:256], T.j8[:], cf(0), None, EQ), ["j8", "cf0"], ["m0"], 128)
+    for z, w in ((T.zq, 68 * C), (T.zc, 36 * C)):
+        for x in range(0, w, 128):
+            y = min(128, w - x)
+            lin("A", z[:, x:x + y, :], T.tiny[:, 0:4 * y], 0.0, 0.0, ["tiny"], ["zero%d_%d" % (w, x)], 4 * y)
+    ZQ, ZC = (["zero%d_%d" % (w, x) for x in range(0, w, 128)] for w in (68 * C, 36 * C))
+    vec(lambda: V.tensor_copy(T.mt[:, 256:512], T.mt[:, 0:256]), ["m0"], ["m1"], 128)
+    vec(lambda: V.tensor_copy(T.mt[:, 512:1024], T.mt[:, 0:512]), ["m0", "m1"], ["m2"], 256)
+    lin("A", T.mt[:, 2048:3072], T.mt[:, 0:1024], 1.0, 0.0, ["m0", "m1", "m2"], ["m4"], 1024)
+    for k in (1, 3): vec(lambda k=k: V.tensor_copy(T.mt[:, 1024 * k:1024 * k + 1024], T.mt[:, 0:1024]), ["m0", "m1", "m2"], ["m%d" % (k + 2)], 512)
+    MT = ["m%d" % k for k in range(6)]
+    sel(T.wx[:], T.onef[:], [[-8, 2], [-16, 8]], GE, 0.0, 0, 1, ["onef"], "wx", 16)
+    sel(T.wx[:], T.wx[:], [[8, 2], [16, 8]], GE, 0.0, 7, -1, ["wx"], "wx", 16)
+    sel(T.im[:], T.nil[:], [[1, 128]], ALU.not_equal, -M, 0, -1, ["nil"], "im", 128)
+    sel(T.wb[:, 0:64], T.one[:, 0:64], [[-2, 8], [-16, 8]], GE, 0.0, 0, 1, ["one"], "wb0", 64)
+    sel(T.wb[:, 64:72], T.one[:, 0:8], [[-16, 8]], GE, 0.0, 0, 1, ["one"], "wb1", 8)
+    sel(T.wb[:, 0:64], T.wb[:, 0:64], [[2, 8], [16, 8]], GE, 0.0, 1, -1, ["wb0"], "wb0", 64)
+    sel(T.wb[:, 64:72], T.wb[:, 64:72], [[16, 8]], GE, 0.0, 15, -1, ["wb1"], "wb1", 8)
+    iota(T.ui[:], [[1, 144]], 0, 0, "ui", 144, True)
+    RI = {}
+    for n in sorted(set(chunks), reverse=True):
+        x = 512 * len(RI); RI[n] = x
+        sel(T.ri[:, x:x + 16 * n], T.pm[:, 256 - 8 * n:256 + 8 * n], [[0, 4], [1, 4 * n]], EQ, 0.0, 0, -1, ["pm0", "pm1"], "ri%d" % n, 16 * n)
+    slot[0] = 2400
+    vec(ts(T.sqh[:], T.sqi[:], -OFF, None, ADD), ["sqi"], ["sqh"], 512)
+    blk = lambda b, q: b[:, 512 * q:512 * q + 512]
+    for q in range(8):
+        slot[0] = cfg["mq"][q]
+        mm([(B[q][:], T.rep[:, 128 * q:128 * q + 128], T.sqh[:], True, False, 512)], ["sqh", "rep%d" % (q // 4)], q, "mq")
+    for q in range(8):
+        slot[0] = cfg["sg"][q]; v = VT[q // 2]; s = "sg%d" % q
+        vec(ts(blk(T.sg, q), blk(T.vt, q), 1.0, -1.0, ALU.min, ALU.max), [v], [s], 256)
+        slot[0] = cfg["tg"][q]
+        if cfg["gq"][q] == "V":
+            mm([(B[q][:], T.ik[:], blk(T.sg, q), False, True, 512)], [s, "ik"], q, "mv")
+            vec(lambda q=q: V.tensor_tensor(blk(T.tg, q), B[q][:], blk(T.vt, q), ADD), [v], ["tg%d" % q], 512, [q])
+        else:
+            mm([(B[q][:], T.idn[:], blk(T.vt, q), False, False, 512), (B[q][:], T.ik[:], blk(T.sg, q), False, True, 512)], [v, s, "idn", "ik"], q, "mv")
+            lin("A", blk(T.tg, q), B[q][:], 1.0, 0.0, [], ["tg%d" % q], 512, [q])
+        slot[0] = cfg["tw"][q]
+        lin(cfg["wq"][q], blk(T.tw, q), blk(T.vt, q), 1.0 / K / UP, 1.0 / UP, [v], ["tw%d" % q], 512)
+    TG, TW = ["tg%d" % q for q in range(8)], ["tw%d" % q for q in range(8)]
+    slot[0] = cfg["late"][0]
+    for j in range(C):
+        n, o = chunks[j], offs[j]
+        vec(lambda n=n, o=o: V.tensor_copy(T.n0[:, 4 * o:4 * o + n], T.le[:, 2 * o:2 * o + 2 * n:2]), ["le0", "le1"], ["n0e%d" % j], n)
+        vec(lambda n=n, o=o: V.tensor_copy(T.n0[:, 4 * o + n:4 * o + 2 * n], T.lf[:, 2 * o:2 * o + 2 * n:2]), ["lf0", "lf1"], ["n0f%d" % j], n)
+        slot[0] += cfg["late"][5]
+    slot[0] = cfg["late"][1]
     vec(ts(T.ci[:, 3:5], T.ki[:, 0:9:8], 112, None, AND), ["ki"], ["ci3"], 1)
     vec(ts(T.ci[:, 6:7], k0, 1, None, AND), ["ki"], ["ci6"], 1)
     vec(ts(T.ci[:, 7:10], T.ki[:, 7:10], 15, None, AND), ["ki"], ["ci7"], 1)
     vec(ts(T.ci[:, 5:6], k0, 14, None, AND), ["ki"], ["ci5"], 1)
     vec(lambda: V.tensor_copy(T.cf[:, 3:10], T.ci[:, 3:10]), ["ci3", "ci5", "ci6", "ci7"], ["cf"], 1)
+    slot[0] = cfg["late"][2]
+    vec(ts(cg(0), cf(6), (W - 1.0) * UP, UP, MUL, ADD), ["cf"], ["cg0"], 1)
     vec(ts(cg(5), cf(4), cf(3), cf(6), SUB, MUL), ["cf"], ["cg5"], 1)
     vec(ts(T.cg[:, 6:9], T.cf[:, 7:10], cf(3), None, ADD), ["cf"], ["cg6"], 1)
+    vec(ts(T.wp[:], T.wb[:], cg(0), None, MUL), ["wb0", "wb1", "cg0"], ["wp"], 36)
+    vec(ts(T.wn[:], T.wb[:], cg(0), -1.0, MUL, MUL), ["wb0", "wb1", "cg0"], ["wn"], 36)
+    slot[0] = cfg["late"][3]
     for d in range(3):
         vec(ts(T.ph[:, 128 * d:128 * d + 128], T.ui[:, 0:128], cg(5), cg(6 + d), SUB, EQ), ["ui", "cg5", "cg6"], ["ph%d" % d], 64)
-    sca(lambda: S.activation(T.pn[:], T.ph[:], ACT.Copy, scale=-1.0), ["ph0", "ph1", "ph2"], ["pn"], 384)
     vec(ts(cg(9), cf(5), cf(3), 1.0, ADD, ADD), ["cf"], ["cg9"], 1)
+    slot[0] = cfg["late"][4]
     vec(ts(cg(10), cg(9), cg(5), None, ADD), ["cg9", "cg5"], ["cg10"], 1)
     vec(ts(cg(11), cf(6), -1.0, 1.0, MUL, ADD), ["cf"], ["cg11"], 1)
+    slot[0] += 2000
     for h in range(2):
         vec(ts(T.zh[:, 144 * h:144 * h + 144], T.ui[:], cg(10), cf(6) if h else cg(11), EQ, MUL), ["ui", "cg10", "cg11", "cf"], ["zh%d" % h], 72)
-    sca(lambda: S.activation(T.zn[:], T.zh[:], ACT.Copy, scale=-1.0), ["zh0", "zh1"], ["zn"], 288)
-    vec(ts(T.old[:], T.one[:], OFF, None, MUL), ["one"], ["top"] + ["old%d" % j for j in range(MAXC)], 256)
-    vec(ts(T.sqh[:], T.sqi[:], -OFF, None, ADD), ["sqi"], ["sqh"], 512)
-    for q in range(8):
-        mm([(B[q][:], T.rep[:, 128 * q:128 * q + 128], T.sqh[:], True, True, 512)], ["sqh", "rep%d" % (q // 4)], q)
-        o = T.qt[:, 512 * q:512 * q + 512]
-        if cfg["qq"][q] == "V": vec(lambda o=o, q=q: V.tensor_copy(o, B[q][:]), [], ["q%d" % q], 512, [q])
-        else: sca(lambda o=o, q=q: S.activation(o, B[q][:], ACT.Copy), [], ["q%d" % q], 512, [q])
-    QT = ["q%d" % q for q in range(8)]
-    for k in range(2):
-        vec(ts(T.wt[:, 2048 * k:2048 * k + 2048], T.vt[:, 2048 * k:2048 * k + 2048], -16.0, None, ADD), ["v%d" % k], ["w%d" % k], 1024)
-    WT = ["w0", "w1"]
-    chunks = cfg["chunks"]; C = len(chunks); offs = [sum(chunks[:j]) for j in range(C)]
-    for j in range(C):
-        n, o = chunks[j], offs[j]
-        vec(lambda n=n, o=o: V.tensor_copy(T.n0[:, 2 * o:2 * o + n], T.le[:, 2 * o:2 * o + 2 * n:2]), ["le0", "le1"], ["n0e%d" % j], n)
-        vec(lambda n=n, o=o: V.tensor_copy(T.n0[:, 2 * o + n:2 * o + 2 * n], T.lf[:, 2 * o:2 * o + 2 * n:2]), ["lf0", "lf1"], ["n0f%d" % j], n)
-    hb, db = cfg["hb"], cfg["db"]
-
-    def sign(side, j, out, in_, r, w, L):
-        if cfg["sign"][(2 * j + side) % len(cfg["sign"])] == "V":
-            vec(ts(out, in_, 1.0, -1.0, ALU.min, ALU.max), [r], [w], L // 2)
-        else:
-            sca(lambda: S.activation(out, in_, ACT.Sign), [r], [w], L)
+    en = cfg["lin"]
 
     def step(t, j):
-        n, o = chunks[j], offs[j]; L = 16 * n; c = max(64, n)
+        n, o = chunks[j], offs[j]; L = 16 * n; c = max(64, n); p = 4 * n; u = t * C + j
         N, SB = T["n%d" % t], T["s%d" % t]
         kE, kF = ("n0e%d" % j, "n0f%d" % j) if t == 0 else ("n%d_%d" % (t, j),) * 2
         big = lambda b: b[:, 16 * o:16 * o + L]
-        sm = lambda b: b[:, 2 * o:2 * o + 2 * n]
-        half = lambda b, h: b[:, 2 * o + h * n:2 * o + h * n + n]
-        part = lambda x: T.tt[:, 4 * o + x * n:4 * o + x * n + n]
-        Ei, Fi = half(N, 0), half(N, 1)
+        cut = lambda b, a: b[:, 16 * o + a:16 * o + L:4]
+        part = lambda b, x, m=1: b[:, 4 * o + x * n:4 * o + (x + m) * n]
         k = lambda s: "%s%d" % (s, j)
-        H = hb[(t * C + j) % len(hb)]; D = db[(t * C + j) % len(db)]
+        X, R, H, Q, D, Y = (cfg[b][u % len(cfg[b])] for b in ("xb", "rb", "hb", "qb", "db", "yb"))
+        rr, fl, zc = T.rr[0:p, 64 * j:64 * j + 64], T.fl[0:p, 256 * j:256 * j + 256], T.zc[0:p, 36 * j + 3:36 * j + 32:4, :]
+        def gather(name, table, x, reads, by=None):
+            halves = [(0, n // 2, "h"), (n // 2, n, "i")]
+            for a, b, keys in ([(a, b, [h]) for a, b, h in halves] if name in cfg["split"] else [(0, n, ["h", "i"])]):
+                win = table[:].indirect(N[:, 4 * o + x * n + a:4 * o + x * n + b]); at = lambda z, a=a, b=b: T[z][:, 16 * (o + a):16 * (o + b)]
+                out = [k(name + h) for h in keys]
+                if name + keys[0] in cfg["scan"]:
+                    gat("a", lambda win=win, at=at: S.activation(at("gw"), win, ACT.Copy), reads, [k("gw" + h) for h in keys], 16 * (b - a))
+                    vec(lambda at=at: V.tensor_tensor_scan(at(name), at(by), at("gw"), 0.0, ADD, MUL), [k(z + h) for z in (by, "gw") for h in keys], out, 16 * (b - a))
+                elif by: gat("v", lambda win=win, at=at: V.tensor_tensor(at(name), win, at(by), MUL), reads + [k(by + h) for h in keys], out, 16 * (b - a))
+                else: gat("a", lambda win=win, at=at: S.activation(at(name), win, ACT.Copy), reads, out, 16 * (b - a))
+            return [k(name + "h"), k(name + "i")]
 
-        def hterm(buf, key, first, last):
-            mm([(B[H][:, 0:4 * n], T.z3[:, 12 - 4 * b:140 - 4 * b], buf[:, 16 * o + b:16 * o + L:4], first and b == 0, last and b == 3, max(64, 4 * n))
-                for b in range(4)], [k(key), "z3"], H, "h" + key)
-
-        def relist(dst, base, own):
-            return [(dst[:, base + w * n:base + w * n + n], T.z2[:, 128 * (2 * w + a):128 * (2 * w + a) + 128],
-                     T.pw[:, 2 * o + a:2 * o + 2 * n:2], own and a == 0, own and a == 1, c) for w in range(2) for a in range(2)]
-
-        gat("a", lambda: S.activation(big(T.mb), T.mt[:].indirect(Fi), ACT.Copy), [kF] + MT, [k("mb")], L)
-        gat("v", lambda: V.tensor_tensor(big(T.xx), T.qt[:].indirect(Ei), big(T.mb), MUL), [kE, k("mb")] + QT, [k("xx")], L)
-        mm([(B[0][:, 0:2 * n], T.z1[:, 7 - b:135 - b], T.xx[:, 16 * o + b:16 * o + L:8], b == 0, b == 7, max(64, 2 * n)) for b in range(8)],
-           [k("xx"), "z1"], 0)
-        vec(ts(sm(T.pw), B[0][:, 0:2 * n], -1.0, None, MUL), [], [k("pw")], 2 * n, [0])
-        mm(relist(B[1], 0, True), [k("pw")] + Z2, 1)
-        vec(ts(sm(T.pl), B[1][:, 0:2 * n], -1.0, OFF, MUL, ADD), [], [k("pl")], 2 * n, [1])
-        gat("a", lambda: S.activation(big(T.ve), T.vt[:].indirect(Ei), ACT.Copy), [kE] + VT, [k("ve")], L)
-        sign(0, j, big(T.se), big(T.ve), k("ve"), k("se"), L)
-        gat("v", lambda: V.tensor_tensor(big(T.pa), T.wt[:].indirect(Fi), big(T.se), MUL), [kF, k("se")] + WT, [k("pa")], L)
-        vec(ts(T.old[:, 4 * o:4 * o + 2 * n], sm(N), -OFF, None, ADD), [kE, kF], [k("old")], n)
-        gat("a", lambda: S.activation(big(T.nv), T.vt[:].indirect(half(T.pl, 0)), ACT.Copy, scale=-1.0), [k("pl")] + VT, [k("nv")], L)
-        sign(1, j, big(T.ns), big(T.nv), k("nv"), k("ns"), L)
-        gat("v", lambda: V.tensor_tensor(big(T.pb), T.wt[:].indirect(half(T.pl, 1)), big(T.ns), MUL), [k("pl"), k("ns")] + WT, [k("pb")], L)
-        hterm(T.ve, "ve", True, False); hterm(T.pa, "pa", False, False)
-        hterm(T.nv, "nv", False, False); hterm(T.pb, "pb", False, True)
-        sca(lambda: S.activation(T.zz[:, 4 * o:4 * o + 4 * n], B[H][:, 0:4 * n], ACT.Abs, scale=2 * OFF), [], [k("zz")], 4 * n, [H])
-        mm([(B[D][:, 0:4 * n], T.ni[:], T.cst[:, 128 - 2 * n:128 + 2 * n], True, False, max(64, 4 * n))] + relist(B[D], 2 * n, False),
-           [k("pw"), "ni", "cst"] + Z2, D, "dl")
-        mm([(B[D][:, w * n:w * n + n], T.z3[:, 12 - 4 * a:140 - 4 * a], T.zz[:, 4 * o + a:4 * o + 4 * n:4], False, w == 3 and a == 3, c)
-            for w in range(4) for a in range(4)], [k("zz"), "z3"], D)
-        vec(lambda: V.tensor_tensor(T.tt[:, 4 * o:4 * o + 4 * n], B[D][:, 0:4 * n], T.old[:, 4 * o:4 * o + 4 * n], ALU.min),
-            [k("old"), "top"], [k("tt")], 4 * n, [D])
+        gather("ge", T.tg, 0, [kE] + TG)
+        xx = gather("xx", T.mt, 1, [kF] + MT, "ge")
+        mm([(B[X][0:p, a:64:4], cut(T.xx, a), T.wx[:], a == 0, a == 3, 256) for a in range(4)], xx + ["wx"], X, "mx")
+        lin(en["rr"], rr, B[X][0:p, 0:64], 1.0, 0.0, [], [k("rr")], 64, [X])
+        vec(lambda: V.tensor_tensor(T.zq[0:p, 68 * j + 3:68 * j + 64:4, :], B[X][0:p, 0:64], rr, SUB), [k("rr")] + ZQ, [k("zq")], 64, [X])
+        mm([(B[R][:, w * n:w * n + n], T.zq[0:p, 68 * j + 32 * w + 3 - h:68 * j + 32 * w + 35 - h, :], T.idn[0:p, h:p:4], h == 0, h == 3, c)
+            for w in range(2) for h in range(4)], [k("zq"), "idn"], R, "ml")
+        lin(en["pl"], part(N, 2, 2), B[R][:, 0:2 * n], FR, OFF, [], ["pl%d_%d" % (t, j)], 2 * n, [R])
+        kP = "pl%d_%d" % (t, j)
+        pa = gather("pa", T.tw, 1, [kF] + TW, "ge")
+        gather("gn", T.tg, 2, [kP] + TG)
+        pb = gather("pb", T.tw, 3, [kP] + TW, "gn")
+        lin(en["old"], part(T.old, 0, 4), part(N, 0, 4), 1.0, -OFF, [kE, kF, kP], [k("old")], 4 * n, narrow=True)
+        mm([(B[H][0:p, a:256:4], cut(T.pa, a), T.wp[:, 0:64], a == 0, False, 64) for a in range(4)], pa + ["wp"], H, "ma")
+        mm([(B[H][0:p, a:256:4], cut(T.pb, a), T.wn[:, 0:64], False, a == 3, 64) for a in range(4)], pb + ["wn"], H, "mb")
+        lin(en["fl"], fl, B[H][0:p, 0:256], 1.0 / M, 191.5 + 0.5 / M, [], [k("fl")], 256, [H])
+        mm([(B[Q][0:p, a:32:4], cut(T.pa, a), T.wp[:, 64:72], a == 0, False, 64) for a in range(4)], pa + ["wp"], Q, "mr")
+        mm([(B[Q][0:p, a:32:4], cut(T.pb, a), T.wn[:, 64:72], False, False, 64) for a in range(4)], pb + ["wn"], Q, "ms")
+        mm([(B[Q][0:p, 0:32], T.im[0:p, 0:p], T.fl[0:p, 256 * j + 32 * i:256 * j + 32 * i + 32], False, i == 7, 64) for i in range(8)],
+           [k("fl"), "im"], Q, "mf")
+        if en["cc"] == "V": vec(ts(zc, B[Q][0:p, 0:32], 0.5 - 8 * 192 * M, 0.5, ALU.is_gt, SUB), ZC, [k("zc")], 32, [Q])
+        else: sca(lambda: S.activation(zc, B[Q][0:p, 0:32], ACT.Sign, bias=8 * 192 * M - 0.5), ZC, [k("zc")], 32, [Q])
+        mm([(B[D][:, 0:4 * n], T.zc[0:p, 36 * j + 3 - h:36 * j + 35 - h, :], T.ri[0:p, RI[n] + h:RI[n] + 16 * n:4], h == 0, h == 3, max(64, 4 * n))
+            for h in range(4)], [k("zc"), "ri%d" % n], D, "mc")
+        vec(lambda: V.tensor_tensor(part(T.tt, 0, 4), B[D][:, 0:4 * n], part(T.old, 0, 4), ALU.min), [k("old")], [k("tt")], 4 * n, [D])
         if t < RO - 1:
-            it, rd = [], ["pn"]
-            for w, d in ((0, 1 if t % 2 == 0 else 2), (1, 0 if t % 2 == 0 else 1)):
-                out = B[7][:, w * n:w * n + n]
-                it += [(out, T.ph[:, 128 * d:128 * d + 128], part(1 - w), True, False, c),
-                       (out, T.pn[:, 128 * d:128 * d + 128], part(3 - w), False, True, c)]
-                rd.append("ph%d" % d)
+            ds = (1 if t % 2 == 0 else 2, 0 if t % 2 == 0 else 1); rd = ["ph%d" % d for d in ds]
+            it = [(B[Y][:, w * n:w * n + n], T.ph[:, 128 * ds[w]:128 * ds[w] + 128], part(T.tt, 2 * x + 1 - w), x == 0, x == 1, c)
+                  for w in range(2) for x in range(2)]
         else:
-            it, rd = [], ["zh0", "zh1", "zn"]
-            for h in range(2):
-                for x in range(4):
-                    y = 144 * h + 1 - x % 2
-                    it.append((B[7][:, h:2 * n:2], (T.zh if x < 2 else T.zn)[:, y:y + 128], part(x), x == 0, x == 3, c))
-        mm(it, rd + [k("tt")], 7, "nx")
-        vec(ts(sm(SB), B[7][:, 0:2 * n], 2 * OFF, None, ADD), [], ["s%d_%d" % (t, j)], 2 * n, [7])
-        i = add("g", lambda: send(sm(T["n%d" % (t + 1)]), sm(SB), T.sem["ar%d_%d" % (t, j)]), ["s%d_%d" % (t, j)], [], cfg["send"], sem="loc", inc=0)
+            rd = ["zh0", "zh1"]
+            it = [(B[Y][:, h:2 * n:2], T.zh[:, 144 * h + 1 - x % 2:144 * h + 129 - x % 2], part(T.tt, x), x == 0, x == 3, c)
+                  for h in range(2) for x in range(4)]
+        mm(it, rd + [k("tt")], Y, "mn")
+        sb = SB[:, 2 * o:2 * o + 2 * n]
+        lin(en["sb"], sb, B[Y][:, 0:2 * n], 1.0, 2 * OFF, [], ["s%d_%d" % (t, j)], 2 * n, [Y])
+        i = add("g", lambda: send(part(T["n%d" % (t + 1)], 0, 2), sb, T.sem["ar%d_%d" % (t, j)]), ["s%d_%d" % (t, j)], [], cfg["send"], sem="loc", inc=0, kind="send")
         add(None, None, [], ["n%d_%d" % (t + 1, j)], 0.0, lat=cfg["fly"], sem="ar%d_%d" % (t, j), inc=cfg["engines"], after=[i])
 
     def last(j):
@@ -254,18 +293,18 @@ def build(g, T, send, cfg):
         end = lambda b: b[:, a + 15:a + L:16]
         for u in range(2):
             x = a + u * 16 * n
-            out, win = T.fw[:, x:x + 16 * n], T.vt[:].indirect(N[:, 2 * o + u * n:2 * o + u * n + n])
+            out, win = T.fw[:, x:x + 16 * n], T.vt[:].indirect(N[:, 4 * o + u * n:4 * o + u * n + n])
             if cfg["fin"][2 * j + u] == "A":
                 gat("a", lambda out=out, win=win: S.activation(out, win, ACT.Identity, bias=-1.0, scale=0.0625), [kN] + VT, [k("fw%d_" % u)], L // 2)
             else:
                 gat("v", ts(out, win, 0.0625, -1.0, MUL, ADD), [kN] + VT, [k("fw%d_" % u)], L // 2)
             vec(ts(T.fs[:, x:x + 16 * n], out, MAGIC, MAGIC - 1.0, ADD, SUB), [k("fw%d_" % u)], [k("fs%d_" % u)], L // 4)
         fw, fs = [k("fw0_"), k("fw1_")], [k("fs0_"), k("fs1_")]
-        vec(lambda: V.tensor_tensor(end(T.fw), end(T.fw), end(T.fs), SUB), fs + fw, fw, 4 * n)
-        vec(lambda: V.memset(end(T.fs), 0.0), [], fs, 2 * n)
+        vec(lambda: V.tensor_tensor(end(T.fw), end(T.fw), end(T.fs), SUB), fs + fw, [k("fe")] + fw, 4 * n)
+        vec(lambda: V.memset(end(T.fs), 0.0), [], [k("fz")] + fs, 2 * n)
         vec(lambda: V.tensor_tensor_scan(rev(T.fu), rev(T.fs), rev(T.fw), 0.0, MUL, ADD), fs + fw, [k("fu")], L // 2)
-        vec(lambda: V.tensor_copy(sm(T.oc), sm(N)), [kN], [k("oc")], 2 * n)
-        sca(lambda: S.activation(sm(T.ob), T.fu[:, a:a + L:16], ACT.Identity, bias=16.0, scale=16.0), [k("fu")], [k("ob")], 2 * n)
+        lin(cfg["oq"][MAXC + j], sm(T.oc), N[:, 4 * o:4 * o + 2 * n], 1.0, 0.0, [kN], [k("oc")], 2 * n)
+        lin(cfg["oq"][j], sm(T.ob), T.fu[:, a:a + L:16], 16.0, 16.0, [k("fu")], [k("ob")], 2 * n)
         dma("s", sm(T.yc), sm(T.oc), [k("oc")], [], "st%d" % (2 * j), 2000)
         dma("s", sm(T.yb), sm(T.ob), [k("ob")], [], "st%d" % (2 * j + 1), 2000)
 
@@ -276,34 +315,18 @@ def build(g, T, send, cfg):
 
 
 def arrange(ops, cfg):
-    n = len(ops); pre = [sorted(o["deps"] | o["order"]) for o in ops]; post = [[] for _ in ops]
-    for i in range(n):
-        for d in pre[i]: post[d].append(i)
-    rank = [0.0] * n
-    for i in range(n - 1, -1, -1):
-        rank[i] = ops[i]["busy"] + ops[i]["lat"] + max([rank[s] + cfg["hop"] for s in post[i]] + [0.0])
-    for i in range(n):
-        rank[i] += cfg["bias"].get(ops[i]["kind"], 0.0) - cfg["beta"] * max(ops[i]["tag"], 0)
-    left = [len(p) for p in pre]; done = [0.0] * n; free = {}; est = {}; seq = []
-
-    def earliest(i):
-        e = 0.0
-        for d in ops[i]["deps"]: e = max(e, done[d] + (cfg["same"] if ops[d]["q"] == ops[i]["q"] else cfg["hop"]))
-        if ops[i]["q"] is None:
-            for d in ops[i]["order"]: e = max(e, done[d])
-        return e
-    for i in range(n):
-        if not left[i]: est[i] = 0.0
-    while est:
-        st = {i: max(e, free.get(ops[i]["q"], 0.0)) if ops[i]["q"] else e for i, e in est.items()}
-        f = min(st, key=lambda i: (st[i], -rank[i])); q = ops[f]["q"]
-        i = max((x for x in st if ops[x]["q"] == q and st[x] <= st[f] + cfg["eps"]), key=lambda x: (rank[x], -x))
-        if q: free[q] = st[i] + ops[i]["busy"]
-        done[i] = st[i] + ops[i]["busy"] + ops[i]["lat"]; seq.append(i); del est[i]
-        for s in post[i]:
+    post = [[] for _ in ops]; left = []
+    for i, o in enumerate(ops):
+        pre = o["deps"] | o["order"]; left.append(len(pre))
+        for d in pre: post[d].append(i)
+    key = [(o["slot"] if o["tag"] < 0 else cfg["start"] + o["tag"] * cfg["period"] + cfg["slots"][o["kind"]], i) for i, o in enumerate(ops)]
+    ready = [key[i] for i in range(len(ops)) if not left[i]]; seq = []
+    while ready:
+        x = min(ready); ready.remove(x); seq.append(x[1])
+        for s in post[x[1]]:
             left[s] -= 1
-            if not left[s]: est[s] = earliest(s)
-    return seq, max(done)
+            if not left[s]: ready.append(key[s])
+    return seq
 
 
 KEPT = {}
@@ -320,7 +343,7 @@ def rank_program(g, core, T, topo):
     mask = sum(1 << e for e in eng)
     send = lambda out, in_, sem: g.remote_dma(out, in_, sem, T.sem.loc, pid, rid, mask)
     ops = build(g, T, send, cfg)
-    if "seq" not in KEPT: KEPT["seq"] = arrange(ops, cfg)[0]
+    if "seq" not in KEPT: KEPT["seq"] = arrange(ops, cfg)
     queue = {"v": g.vector, "a": g.scalar, "p": g.tensor, "g": g, "s": g.sync}
     known = {q: {} for q in queue}; total = {}; mark = {}; carry = {}
     for i in KEPT["seq"]:

from concourse.mybir import AluOpType, ActivationFunctionType

ALU = AluOpType
ACT = ActivationFunctionType
E, RO = 4096, 5
CFG = {
    "chunks": [28, 28, 24, 24, 24],
    "lin": {"rr": "V", "pl": "A", "old": "A", "sb": "V", "fl": "A", "cc": "V"},
    "gq": "AVAAVVAV", "wq": "AAAAAAVA", "fin": "AAAAAAAVAAVA",
    "xb": [0], "rb": [1], "hb": [2, 3], "qb": [4, 5], "db": [6], "yb": [7],
    "engines": 16,
    "mq": [3600, 4400, -100, 3900, 5700, 3900, 1900, 4900], "tw": [2000, 0, 3600, 5000, 8500, 8500, 8800, 8800],
    "late": [4500, 1000, 9000, 10000, 14000], "start": 7800, "period": 2300,
    "slots": {'ge': -300, 'xx': 1550, 'mx': 2460, 'rr': 3270, 'zq': 3280, 'ml': 3520, 'pl': 4230, 'gn': 4240, 'pb': 5250, 'mb': 5510, 'fl': 6320, 'mf': 6330, 'zc': 7040, 'mc': 7650, 'tt': 8110, 'mn': 8520, 's': 9160, 'send': 11370, 'n': 11780, 'pa': 3400, 'ma': 4500, 'old': 5000, 'mr': 4510, 'ms': 5520, 'fw': -3800, 'fs': 3500, 'fe': 3510, 'fz': 4520, 'fu': 4530, 'oc': 1800, 'ob': 5040, 'out': 5550},
    "lat": {"p": 100.0, "a": 80.0}, "g": 1.56, "f": 1.05, "pe": 0.42, "hop": 130.0, "same": 40.0, "send": 400.0, "fly": 1400.0,
    "ov": 10, "oa": 50,
}
CFG.update({'chunks': [28, 28, 24, 24, 24], 'lin': {'rr': 'A', 'pl': 'A', 'old': 'A', 'sb': 'V', 'fl': 'A', 'cc': 'A'}, 'gq': 'VVAAVVAV', 'wq': 'AAAAVVAA', 'fin': 'AVVAAAAAAAAA', 'mq': [4100, 1400, -1400, 4900, 5700, 1900, 1000, -2300], 'tw': [3900, 1700, 7500, 1600, 7100, 8700, 3300, 4700], 'late': [6200, 2000, 7000, 12500, 16400], 'start': 5100, 'period': 2250, 'slots': {'ge': 1000, 'xx': 2310, 'mx': 3720, 'rr': 3930, 'zq': 4040, 'ml': 5090, 'pl': 5600, 'gn': 5710, 'pb': 6220, 'mb': 6820, 'fl': 7830, 'mf': 8130, 'zc': 8240, 'mc': 8650, 'tt': 8960, 'mn': 9820, 's': 9830, 'send': 13240, 'n': 13550, 'pa': 5200, 'ma': 6810, 'old': 7140, 'mr': 6810, 'ms': 8120, 'fw': -2400, 'fs': 4600, 'fe': 6210, 'fz': 6220, 'fu': 6230, 'oc': -9600, 'ob': 11640, 'out': 12850}})
CFG["split"] = ["ge", "xx", "gn", "pb"]; CFG["scan"] = []
CFG.update({"sg": [3300, 3350, 4000, 4050, 4700, 4750, 5400, 5450], "tg": [4000, 4300, 4700, 5000, 5400, 5700, 6100, 6200], "oq": "AAAVVVAAAAAA"})
CFG.update({'chunks': [28, 28, 24, 24, 24], 'lin': {'rr': 'V', 'pl': 'A', 'old': 'A', 'sb': 'A', 'fl': 'A', 'cc': 'V'}, 'gq': 'AAAAVVAV', 'wq': 'VAAAAAVA', 'fin': 'VAAAAAAVAVAA', 'mq': [1800, 2700, -2000, 3500, 6000, -1300, -1100, 4900], 'tw': [5300, 0, 1700, 4700, 7900, 9600, 7700, 9800], 'late': [6000, 1000, 4500, 9200, 16600], 'start': 8100, 'period': 2300, 'slots': {'geh': 100.0, 'gei': 800.0, 'xxh': 110.0, 'xxi': 810.0, 'mx': 1720.0, 'rr': 1930.0, 'zq': 2240.0, 'ml': 2950.0, 'pl': 3410.0, 'gnh': 4140.0, 'gni': 4540.0, 'pbh': 4150.0, 'pbi': 4550.0, 'mb': 5640.0, 'fl': 5850.0, 'ms': 5730.0, 'mf': 6500.0, 'zc': 6610.0, 'mc': 7420.0, 'tt': 7690.0, 'mn': 8200.0, 's': 8810.0, 'send': 8920.0, 'n': 10830.0, 'pah': 810.0, 'pai': -990.0, 'ma': 2100.0, 'mr': 5720.0, 'old': 7180.0, 'fw': 900.0, 'fs': 1110.0, 'fe': 1720.0, 'fz': 2260.0, 'fu': 3070.0, 'oc': 7450.0, 'ob': 3620.0, 'out': 17530.0}})
CFG.update({'chunks': [28, 28, 24, 24, 24], 'split': ['ge', 'xx', 'gn', 'pb', 'pa'], 'scan': ['pai'], 'sg': [2600, 3050, 4000, 4050, 4300, 4050, 4800, 5450], 'tg': [1700, 3350, 6500, 1250, 5500, 3550, 5700, 6550], 'oq': 'VAAAVAAVVAVA', 'lin': {'rr': 'V', 'pl': 'A', 'old': 'A', 'sb': 'V', 'fl': 'A', 'cc': 'V'}, 'gq': 'VAVAVAVA', 'wq': 'AAAAAVAA', 'fin': 'AVAAAAAAVAVA', 'mq': [8200, 2900, -3900, 4000, 3900, 6300, -300, 4500], 'tw': [500, 4500, 2200, 3600, 6100, 9100, 5500, 10300], 'late': [6300, 3800, 4800, 11000, 17900, 1000], 'start': 11100, 'period': 2300, 'slots': {'geh': -2500, 'gei': -2800, 'xxh': -490, 'xxi': -510, 'mx': 1200, 'rr': 1310, 'zq': 1620, 'ml': 2130, 'pl': 3560, 'gnh': 3570, 'gni': 3670, 'pbh': 3580, 'pbi': 4080, 'mb': 5070, 'fl': 5880, 'ms': 5270, 'mf': 5990, 'zc': 6390, 'mc': 7280, 'tt': 7290, 'mn': 8200, 's': 8510, 'send': 9420, 'n': 11630, 'gwh': 20, 'gwi': 640, 'pah': 710, 'pai': 2550, 'ma': 3960, 'mr': 3760, 'old': 6550, 'fw': -3600, 'fs': 2310, 'fe': 2320, 'fz': 2330, 'fu': 2740, 'oc': 4150, 'ob': 5020, 'out': 5430}})
MAXC = 6
OFF = 2048.0
MAGIC = 12582912.0
K = 1984.0
M = 2 * K
W = 61.0
UP = 2.0 ** 20
FR = 8192.0


def _sb(n, dt):
    return ("sbuf", [128, n], dt)


SCRATCH = {
    "vt": _sb(E, "bfloat16"), "sg": _sb(E, "bfloat16"), "mt": _sb(E, "bfloat16"), "tg": _sb(E, "float32"), "tw": _sb(E, "float32"),
    "sqi": _sb(512, "int32"), "sqh": _sb(512, "float16"), "le": _sb(256, "int32"), "lf": _sb(256, "int32"),
    "ki": _sb(16, "int32"), "ci": _sb(16, "int32"), "cf": _sb(16, "float32"), "cg": _sb(16, "float32"),
    "one": _sb(64, "bfloat16"), "pm": _sb(512, "bfloat16"), "tiny": _sb(512, "bfloat16"), "nil": _sb(128, "bfloat16"), "j8": _sb(256, "bfloat16"),
    "ui": _sb(144, "bfloat16"), "onef": _sb(16, "float32"), "wx": _sb(16, "float32"), "wb": _sb(72, "bfloat16"),
    "wp": _sb(72, "bfloat16"), "wn": _sb(72, "bfloat16"), "rep": _sb(1024, "bfloat16"), "idn": _sb(128, "bfloat16"),
    "ik": _sb(128, "bfloat16"), "im": _sb(128, "bfloat16"),
    "ri": _sb(1536, "bfloat16"), "ph": _sb(384, "bfloat16"), "zh": _sb(288, "bfloat16"),
    "ge": _sb(2048, "float32"), "gw": _sb(2048, "float32"), "gn": _sb(2048, "float32"), "xx": _sb(2048, "float32"), "pa": _sb(2048, "float16"), "pb": _sb(2048, "float16"),
    "rr": _sb(64 * MAXC, "float16"), "fl": _sb(256 * MAXC, "bfloat16"),
    "zq": ("sbuf", [128, 68 * MAXC, 4], "float16"), "zc": ("sbuf", [128, 36 * MAXC, 4], "bfloat16"),
    "old": _sb(512, "float16"),
    "tt": _sb(512, "float16"), "fw": _sb(E, "bfloat16"), "fs": _sb(E, "bfloat16"), "fu": _sb(E, "bfloat16"),
    "oc": _sb(256, "float32"), "ob": _sb(256, "float32"),
}
for _t in range(RO + 1):
    SCRATCH["n%d" % _t] = _sb(512, "uint16")
for _t in range(RO):
    SCRATCH["s%d" % _t] = _sb(256, "uint16")
for _t in range(8):
    SCRATCH["b%d" % _t] = ("psum", [128, 512], "float32")
SEMAPHORES = (["cv", "ca", "cp", "cg", "loc"] + ["ld%d" % k for k in range(10)] + ["st%d" % k for k in range(2 * MAXC)]
              + ["ar%d_%d" % (t, j) for t in range(RO) for j in range(MAXC)])
COUNTER = {"v": "cv", "a": "ca", "p": "cp", "g": "cg"}


def build(g, T, send, cfg):
    ops, lastw, readers, bank, tag, slot = [], {}, {}, {}, [-1], [0]
    cyc = 0.83 * cfg["f"]
    V, S, P = g.vector, g.scalar, g.tensor
    EQ, GE, MUL, ADD, SUB, AND = ALU.is_equal, ALU.is_ge, ALU.mult, ALU.add, ALU.subtract, ALU.bitwise_and

    def add(q, fn, reads, writes, busy, banks=(), lat=0.0, sem=None, inc=1, after=(), kind=None):
        i = len(ops); deps = set(); order = set(after)
        for r in reads:
            if r in lastw: deps.add(lastw[r])
        for w in writes:
            if w in lastw: deps.add(lastw[w])
            deps.update(readers.get(w, ()))
        for r in reads: readers.setdefault(r, []).append(i)
        for w in writes: lastw[w] = i; readers[w] = []
        for b in banks:
            cur, prev = bank.get(b, ([], []))
            if cur and ops[cur[-1]]["q"] == q:
                deps.update(prev); order.add(cur[-1]); bank[b] = (cur + [i], prev)
            else:
                deps.update(cur); bank[b] = ([i], cur)
        deps.discard(i)
        if sem is None: lat += cfg["lat"].get(q, 0.0)
        ops.append({"q": q, "fn": fn, "deps": deps, "order": order, "busy": busy, "lat": lat, "sem": sem, "inc": inc, "tag": tag[0], "slot": slot[0],
                    "kind": kind or "".join(x for x in (list(writes) + ["out"])[0] if x.isalpha())})
        return i

    def vec(fn, reads, writes, n, banks=()):
        return add("v", fn, reads, writes, cfg["ov"] + max(64, n) * cyc, banks)

    def sca(fn, reads, writes, n, banks=()):
        return add("a", fn, reads, writes, cfg["oa"] + max(64, n) * cyc, banks)

    def gat(q, fn, reads, writes, n):
        return add(q, fn, reads, writes, (50 if q == "v" else 65) + n * cfg["g"] * cyc)

    def mm(items, reads, b, kind):
        def fn():
            r = None
            for o, l, x, st, sp, c in items: r = P.matmul(o, l, x, st, sp)
            return r
        return add("p", fn, reads, [], 30 + sum(it[5] for it in items) * cfg["pe"] * cfg["f"], [b], kind=kind)

    def dma(q, out, in_, reads, writes, sem, lat):
        e = g.sync if q == "s" else S
        return add(q, lambda: e.dma_start(out, in_), reads, writes, 60.0, lat=lat * cfg.get("ld", 1.0), sem=sem, inc=16)

    def ts(out, in0, a, b, o0, o1=None):
        if o1 is None: return lambda: V.tensor_scalar(out, in0, a, None, o0)
        return lambda: V.tensor_scalar(out, in0, a, b, o0, o1)

    def lin(e, out, in_, scale, bias, reads, writes, n, banks=(), narrow=False):
        if e == "V": return vec(ts(out, in_, scale, bias, MUL, ADD), reads, writes, n // 2 if narrow else n, banks)
        return sca(lambda: S.activation(out, in_, ACT.Identity, bias=bias, scale=scale), reads, writes, n, banks)

    def iota(out, pat, base, cm, key, n, small):
        if small: fn = lambda: g.iota(out, pat, base, cm, allow_small_or_imprecise_dtypes=True)
        else: fn = lambda: g.iota(out, pat, base, cm)
        return add("g", fn, [], [key], 130 + 2 * n * cyc)

    def sel(out, in_, pat, op, fill, base, cm, reads, key, n):
        return add("g", lambda: g.affine_select(out, in_, pat, op, fill, base, cm), reads, [key], 170 + 2 * n * cyc)

    B = [T["b%d" % k] for k in range(8)]
    chunks = cfg["chunks"]; C = len(chunks); offs = [sum(chunks[:j]) for j in range(C)]
    dma("s", T.sqi[:], T.sq[:], [], ["sqi"], "ld0", 2600)
    for k in range(4):
        dma("as"[k % 2], T.vt[:, 1024 * k:1024 * k + 1024], T.v[:, 1024 * k:1024 * k + 1024], [], ["v%d" % k], "ld%d" % (5 + k), 3300 + 700 * k)
    VT = ["v%d" % k for k in range(4)]
    dma("a", T.le[0::2, :], T.lp[0::2, :], [], ["le0"], "ld1", 5600)
    dma("s", T.le[1::2, 0:255], T.lp[0::2, 1:256], [], ["le1"], "ld2", 5700)
    dma("a", T.lf[0::2, :], T.lp[1::2, :], [], ["lf0"], "ld3", 5800)
    dma("s", T.lf[1::2, 0:255], T.lp[1::2, 1:256], [], ["lf1"], "ld4", 5900)
    k0 = T.ki[:, 0:1]
    cf = lambda k: T.cf[:, k:k + 1]
    cg = lambda k: T.cg[:, k:k + 1]
    iota(T.ki[:, 0:10], [[2, 10]], 0, 1, "ki", 10, False)
    iota(T.j8[:], [[0, 32], [1, 8]], 0, 0, "j8", 256, True)
    vec(lambda: V.memset(T.tiny[:], 1.0 / FR), [], ["tiny"], 256)
    vec(lambda: V.memset(T.nil[:], 0.0), [], ["nil"], 64)
    vec(ts(T.ci[:, 0:1], k0, 7, None, AND), ["ki"], ["ci0"], 1)
    vec(lambda: V.memset(T.one[:], 1.0), [], ["one"], 32)
    y = 2 * OFF if cfg["lin"]["cc"] == "V" else OFF
    for u in range(2): vec(lambda u=u, y=y: V.memset(T.pm[:, 256 * u:256 * u + 256], y - 2 * u * y), [], ["pm%d" % u], 128)
    vec(lambda: V.tensor_copy(cf(0), T.ci[:, 0:1]), ["ci0"], ["cf0"], 1)
    vec(lambda: V.memset(T.onef[:], 1.0), [], ["onef"], 16)
    for u in range(2):
        sel(T.rep[:, 512 * u:512 * u + 512], T.tiny[:], [[1, 4], [0, 8], [8, 16]], EQ, 0.0, 4 * u, -1, ["tiny"], "rep%d" % u, 512)
    for name, x in (("ik", K - 16), ("idn", 1.0)):
        sel(T[name][:], T.nil[:], [[1, 128]], ALU.not_equal, x, 0, -1, ["nil"], name, 128)
    vec(ts(T.mt[:, 0:256], T.j8[:], cf(0), None, EQ), ["j8", "cf0"], ["m0"], 128)
    for z, w in ((T.zq, 68 * C), (T.zc, 36 * C)):
        for x in range(0, w, 128):
            y = min(128, w - x)
            lin("A", z[:, x:x + y, :], T.tiny[:, 0:4 * y], 0.0, 0.0, ["tiny"], ["zero%d_%d" % (w, x)], 4 * y)
    ZQ, ZC = (["zero%d_%d" % (w, x) for x in range(0, w, 128)] for w in (68 * C, 36 * C))
    vec(lambda: V.tensor_copy(T.mt[:, 256:512], T.mt[:, 0:256]), ["m0"], ["m1"], 128)
    vec(lambda: V.tensor_copy(T.mt[:, 512:1024], T.mt[:, 0:512]), ["m0", "m1"], ["m2"], 256)
    lin("A", T.mt[:, 2048:3072], T.mt[:, 0:1024], 1.0, 0.0, ["m0", "m1", "m2"], ["m4"], 1024)
    for k in (1, 3): vec(lambda k=k: V.tensor_copy(T.mt[:, 1024 * k:1024 * k + 1024], T.mt[:, 0:1024]), ["m0", "m1", "m2"], ["m%d" % (k + 2)], 512)
    MT = ["m%d" % k for k in range(6)]
    sel(T.wx[:], T.onef[:], [[-8, 2], [-16, 8]], GE, 0.0, 0, 1, ["onef"], "wx", 16)
    sel(T.wx[:], T.wx[:], [[8, 2], [16, 8]], GE, 0.0, 7, -1, ["wx"], "wx", 16)
    sel(T.im[:], T.nil[:], [[1, 128]], ALU.not_equal, -M, 0, -1, ["nil"], "im", 128)
    sel(T.wb[:, 0:64], T.one[:, 0:64], [[-2, 8], [-16, 8]], GE, 0.0, 0, 1, ["one"], "wb0", 64)
    sel(T.wb[:, 64:72], T.one[:, 0:8], [[-16, 8]], GE, 0.0, 0, 1, ["one"], "wb1", 8)
    sel(T.wb[:, 0:64], T.wb[:, 0:64], [[2, 8], [16, 8]], GE, 0.0, 1, -1, ["wb0"], "wb0", 64)
    sel(T.wb[:, 64:72], T.wb[:, 64:72], [[16, 8]], GE, 0.0, 15, -1, ["wb1"], "wb1", 8)
    iota(T.ui[:], [[1, 144]], 0, 0, "ui", 144, True)
    RI = {}
    for n in sorted(set(chunks), reverse=True):
        x = 512 * len(RI); RI[n] = x
        sel(T.ri[:, x:x + 16 * n], T.pm[:, 256 - 8 * n:256 + 8 * n], [[0, 4], [1, 4 * n]], EQ, 0.0, 0, -1, ["pm0", "pm1"], "ri%d" % n, 16 * n)
    slot[0] = 2400
    vec(ts(T.sqh[:], T.sqi[:], -OFF, None, ADD), ["sqi"], ["sqh"], 512)
    blk = lambda b, q: b[:, 512 * q:512 * q + 512]
    for q in range(8):
        slot[0] = cfg["mq"][q]
        mm([(B[q][:], T.rep[:, 128 * q:128 * q + 128], T.sqh[:], True, False, 512)], ["sqh", "rep%d" % (q // 4)], q, "mq")
    for q in range(8):
        slot[0] = cfg["sg"][q]; v = VT[q // 2]; s = "sg%d" % q
        vec(ts(blk(T.sg, q), blk(T.vt, q), 1.0, -1.0, ALU.min, ALU.max), [v], [s], 256)
        slot[0] = cfg["tg"][q]
        if cfg["gq"][q] == "V":
            mm([(B[q][:], T.ik[:], blk(T.sg, q), False, True, 512)], [s, "ik"], q, "mv")
            vec(lambda q=q: V.tensor_tensor(blk(T.tg, q), B[q][:], blk(T.vt, q), ADD), [v], ["tg%d" % q], 512, [q])
        else:
            mm([(B[q][:], T.idn[:], blk(T.vt, q), False, False, 512), (B[q][:], T.ik[:], blk(T.sg, q), False, True, 512)], [v, s, "idn", "ik"], q, "mv")
            lin("A", blk(T.tg, q), B[q][:], 1.0, 0.0, [], ["tg%d" % q], 512, [q])
        slot[0] = cfg["tw"][q]
        lin(cfg["wq"][q], blk(T.tw, q), blk(T.vt, q), 1.0 / K / UP, 1.0 / UP, [v], ["tw%d" % q], 512)
    TG, TW = ["tg%d" % q for q in range(8)], ["tw%d" % q for q in range(8)]
    slot[0] = cfg["late"][0]
    for j in range(C):
        n, o = chunks[j], offs[j]
        vec(lambda n=n, o=o: V.tensor_copy(T.n0[:, 4 * o:4 * o + n], T.le[:, 2 * o:2 * o + 2 * n:2]), ["le0", "le1"], ["n0e%d" % j], n)
        vec(lambda n=n, o=o: V.tensor_copy(T.n0[:, 4 * o + n:4 * o + 2 * n], T.lf[:, 2 * o:2 * o + 2 * n:2]), ["lf0", "lf1"], ["n0f%d" % j], n)
        slot[0] += cfg["late"][5]
    slot[0] = cfg["late"][1]
    vec(ts(T.ci[:, 3:5], T.ki[:, 0:9:8], 112, None, AND), ["ki"], ["ci3"], 1)
    vec(ts(T.ci[:, 6:7], k0, 1, None, AND), ["ki"], ["ci6"], 1)
    vec(ts(T.ci[:, 7:10], T.ki[:, 7:10], 15, None, AND), ["ki"], ["ci7"], 1)
    vec(ts(T.ci[:, 5:6], k0, 14, None, AND), ["ki"], ["ci5"], 1)
    vec(lambda: V.tensor_copy(T.cf[:, 3:10], T.ci[:, 3:10]), ["ci3", "ci5", "ci6", "ci7"], ["cf"], 1)
    slot[0] = cfg["late"][2]
    vec(ts(cg(0), cf(6), (W - 1.0) * UP, UP, MUL, ADD), ["cf"], ["cg0"], 1)
    vec(ts(cg(5), cf(4), cf(3), cf(6), SUB, MUL), ["cf"], ["cg5"], 1)
    vec(ts(T.cg[:, 6:9], T.cf[:, 7:10], cf(3), None, ADD), ["cf"], ["cg6"], 1)
    vec(ts(T.wp[:], T.wb[:], cg(0), None, MUL), ["wb0", "wb1", "cg0"], ["wp"], 36)
    vec(ts(T.wn[:], T.wb[:], cg(0), -1.0, MUL, MUL), ["wb0", "wb1", "cg0"], ["wn"], 36)
    slot[0] = cfg["late"][3]
    for d in range(3):
        vec(ts(T.ph[:, 128 * d:128 * d + 128], T.ui[:, 0:128], cg(5), cg(6 + d), SUB, EQ), ["ui", "cg5", "cg6"], ["ph%d" % d], 64)
    vec(ts(cg(9), cf(5), cf(3), 1.0, ADD, ADD), ["cf"], ["cg9"], 1)
    slot[0] = cfg["late"][4]
    vec(ts(cg(10), cg(9), cg(5), None, ADD), ["cg9", "cg5"], ["cg10"], 1)
    vec(ts(cg(11), cf(6), -1.0, 1.0, MUL, ADD), ["cf"], ["cg11"], 1)
    slot[0] += 2000
    for h in range(2):
        vec(ts(T.zh[:, 144 * h:144 * h + 144], T.ui[:], cg(10), cf(6) if h else cg(11), EQ, MUL), ["ui", "cg10", "cg11", "cf"], ["zh%d" % h], 72)
    en = cfg["lin"]

    def step(t, j):
        n, o = chunks[j], offs[j]; L = 16 * n; c = max(64, n); p = 4 * n; u = t * C + j
        N, SB = T["n%d" % t], T["s%d" % t]
        kE, kF = ("n0e%d" % j, "n0f%d" % j) if t == 0 else ("n%d_%d" % (t, j),) * 2
        big = lambda b: b[:, 16 * o:16 * o + L]
        cut = lambda b, a: b[:, 16 * o + a:16 * o + L:4]
        part = lambda b, x, m=1: b[:, 4 * o + x * n:4 * o + (x + m) * n]
        k = lambda s: "%s%d" % (s, j)
        X, R, H, Q, D, Y = (cfg[b][u % len(cfg[b])] for b in ("xb", "rb", "hb", "qb", "db", "yb"))
        rr, fl, zc = T.rr[0:p, 64 * j:64 * j + 64], T.fl[0:p, 256 * j:256 * j + 256], T.zc[0:p, 36 * j + 3:36 * j + 32:4, :]
        def gather(name, table, x, reads, by=None):
            halves = [(0, n // 2, "h"), (n // 2, n, "i")]
            for a, b, keys in ([(a, b, [h]) for a, b, h in halves] if name in cfg["split"] else [(0, n, ["h", "i"])]):
                win = table[:].indirect(N[:, 4 * o + x * n + a:4 * o + x * n + b]); at = lambda z, a=a, b=b: T[z][:, 16 * (o + a):16 * (o + b)]
                out = [k(name + h) for h in keys]
                if name + keys[0] in cfg["scan"]:
                    gat("a", lambda win=win, at=at: S.activation(at("gw"), win, ACT.Copy), reads, [k("gw" + h) for h in keys], 16 * (b - a))
                    vec(lambda at=at: V.tensor_tensor_scan(at(name), at(by), at("gw"), 0.0, ADD, MUL), [k(z + h) for z in (by, "gw") for h in keys], out, 16 * (b - a))
                elif by: gat("v", lambda win=win, at=at: V.tensor_tensor(at(name), win, at(by), MUL), reads + [k(by + h) for h in keys], out, 16 * (b - a))
                else: gat("a", lambda win=win, at=at: S.activation(at(name), win, ACT.Copy), reads, out, 16 * (b - a))
            return [k(name + "h"), k(name + "i")]

        gather("ge", T.tg, 0, [kE] + TG)
        xx = gather("xx", T.mt, 1, [kF] + MT, "ge")
        mm([(B[X][0:p, a:64:4], cut(T.xx, a), T.wx[:], a == 0, a == 3, 256) for a in range(4)], xx + ["wx"], X, "mx")
        lin(en["rr"], rr, B[X][0:p, 0:64], 1.0, 0.0, [], [k("rr")], 64, [X])
        vec(lambda: V.tensor_tensor(T.zq[0:p, 68 * j + 3:68 * j + 64:4, :], B[X][0:p, 0:64], rr, SUB), [k("rr")] + ZQ, [k("zq")], 64, [X])
        mm([(B[R][:, w * n:w * n + n], T.zq[0:p, 68 * j + 32 * w + 3 - h:68 * j + 32 * w + 35 - h, :], T.idn[0:p, h:p:4], h == 0, h == 3, c)
            for w in range(2) for h in range(4)], [k("zq"), "idn"], R, "ml")
        lin(en["pl"], part(N, 2, 2), B[R][:, 0:2 * n], FR, OFF, [], ["pl%d_%d" % (t, j)], 2 * n, [R])
        kP = "pl%d_%d" % (t, j)
        pa = gather("pa", T.tw, 1, [kF] + TW, "ge")
        gather("gn", T.tg, 2, [kP] + TG)
        pb = gather("pb", T.tw, 3, [kP] + TW, "gn")
        lin(en["old"], part(T.old, 0, 4), part(N, 0, 4), 1.0, -OFF, [kE, kF, kP], [k("old")], 4 * n, narrow=True)
        mm([(B[H][0:p, a:256:4], cut(T.pa, a), T.wp[:, 0:64], a == 0, False, 64) for a in range(4)], pa + ["wp"], H, "ma")
        mm([(B[H][0:p, a:256:4], cut(T.pb, a), T.wn[:, 0:64], False, a == 3, 64) for a in range(4)], pb + ["wn"], H, "mb")
        lin(en["fl"], fl, B[H][0:p, 0:256], 1.0 / M, 191.5 + 0.5 / M, [], [k("fl")], 256, [H])
        mm([(B[Q][0:p, a:32:4], cut(T.pa, a), T.wp[:, 64:72], a == 0, False, 64) for a in range(4)], pa + ["wp"], Q, "mr")
        mm([(B[Q][0:p, a:32:4], cut(T.pb, a), T.wn[:, 64:72], False, False, 64) for a in range(4)], pb + ["wn"], Q, "ms")
        mm([(B[Q][0:p, 0:32], T.im[0:p, 0:p], T.fl[0:p, 256 * j + 32 * i:256 * j + 32 * i + 32], False, i == 7, 64) for i in range(8)],
           [k("fl"), "im"], Q, "mf")
        if en["cc"] == "V": vec(ts(zc, B[Q][0:p, 0:32], 0.5 - 8 * 192 * M, 0.5, ALU.is_gt, SUB), ZC, [k("zc")], 32, [Q])
        else: sca(lambda: S.activation(zc, B[Q][0:p, 0:32], ACT.Sign, bias=8 * 192 * M - 0.5), ZC, [k("zc")], 32, [Q])
        mm([(B[D][:, 0:4 * n], T.zc[0:p, 36 * j + 3 - h:36 * j + 35 - h, :], T.ri[0:p, RI[n] + h:RI[n] + 16 * n:4], h == 0, h == 3, max(64, 4 * n))
            for h in range(4)], [k("zc"), "ri%d" % n], D, "mc")
        vec(lambda: V.tensor_tensor(part(T.tt, 0, 4), B[D][:, 0:4 * n], part(T.old, 0, 4), ALU.min), [k("old")], [k("tt")], 4 * n, [D])
        if t < RO - 1:
            ds = (1 if t % 2 == 0 else 2, 0 if t % 2 == 0 else 1); rd = ["ph%d" % d for d in ds]
            it = [(B[Y][:, w * n:w * n + n], T.ph[:, 128 * ds[w]:128 * ds[w] + 128], part(T.tt, 2 * x + 1 - w), x == 0, x == 1, c)
                  for w in range(2) for x in range(2)]
        else:
            rd = ["zh0", "zh1"]
            it = [(B[Y][:, h:2 * n:2], T.zh[:, 144 * h + 1 - x % 2:144 * h + 129 - x % 2], part(T.tt, x), x == 0, x == 3, c)
                  for h in range(2) for x in range(4)]
        mm(it, rd + [k("tt")], Y, "mn")
        sb = SB[:, 2 * o:2 * o + 2 * n]
        lin(en["sb"], sb, B[Y][:, 0:2 * n], 1.0, 2 * OFF, [], ["s%d_%d" % (t, j)], 2 * n, [Y])
        i = add("g", lambda: send(part(T["n%d" % (t + 1)], 0, 2), sb, T.sem["ar%d_%d" % (t, j)]), ["s%d_%d" % (t, j)], [], cfg["send"], sem="loc", inc=0, kind="send")
        add(None, None, [], ["n%d_%d" % (t + 1, j)], 0.0, lat=cfg["fly"], sem="ar%d_%d" % (t, j), inc=cfg["engines"], after=[i])

    def last(j):
        n, o = chunks[j], offs[j]; L = 32 * n; a = 32 * o
        N = T["n%d" % RO]; kN = "n%d_%d" % (RO, j)
        k = lambda s: "%s%d" % (s, j)
        sm = lambda b: b[:, 2 * o:2 * o + 2 * n]
        rev = lambda b: b[:, a + L - 1:a - 1:-1] if a else b[:, L - 1::-1]
        end = lambda b: b[:, a + 15:a + L:16]
        for u in range(2):
            x = a + u * 16 * n
            out, win = T.fw[:, x:x + 16 * n], T.vt[:].indirect(N[:, 4 * o + u * n:4 * o + u * n + n])
            if cfg["fin"][2 * j + u] == "A":
                gat("a", lambda out=out, win=win: S.activation(out, win, ACT.Identity, bias=-1.0, scale=0.0625), [kN] + VT, [k("fw%d_" % u)], L // 2)
            else:
                gat("v", ts(out, win, 0.0625, -1.0, MUL, ADD), [kN] + VT, [k("fw%d_" % u)], L // 2)
            vec(ts(T.fs[:, x:x + 16 * n], out, MAGIC, MAGIC - 1.0, ADD, SUB), [k("fw%d_" % u)], [k("fs%d_" % u)], L // 4)
        fw, fs = [k("fw0_"), k("fw1_")], [k("fs0_"), k("fs1_")]
        vec(lambda: V.tensor_tensor(end(T.fw), end(T.fw), end(T.fs), SUB), fs + fw, [k("fe")] + fw, 4 * n)
        vec(lambda: V.memset(end(T.fs), 0.0), [], [k("fz")] + fs, 2 * n)
        vec(lambda: V.tensor_tensor_scan(rev(T.fu), rev(T.fs), rev(T.fw), 0.0, MUL, ADD), fs + fw, [k("fu")], L // 2)
        lin(cfg["oq"][MAXC + j], sm(T.oc), N[:, 4 * o:4 * o + 2 * n], 1.0, 0.0, [kN], [k("oc")], 2 * n)
        lin(cfg["oq"][j], sm(T.ob), T.fu[:, a:a + L:16], 16.0, 16.0, [k("fu")], [k("ob")], 2 * n)
        dma("s", sm(T.yc), sm(T.oc), [k("oc")], [], "st%d" % (2 * j), 2000)
        dma("s", sm(T.yb), sm(T.ob), [k("ob")], [], "st%d" % (2 * j + 1), 2000)

    for t in range(RO):
        for j in range(C): tag[0] = t * C + j; step(t, j)
    for j in range(C): tag[0] = RO * C + j; last(j)
    return ops


def arrange(ops, cfg):
    post = [[] for _ in ops]; left = []
    for i, o in enumerate(ops):
        pre = o["deps"] | o["order"]; left.append(len(pre))
        for d in pre: post[d].append(i)
    key = [(o["slot"] if o["tag"] < 0 else cfg["start"] + o["tag"] * cfg["period"] + cfg["slots"][o["kind"]], i) for i, o in enumerate(ops)]
    ready = [key[i] for i in range(len(ops)) if not left[i]]; seq = []
    while ready:
        x = min(ready); ready.remove(x); seq.append(x[1])
        for s in post[x[1]]:
            left[s] -= 1
            if not left[s]: ready.append(key[s])
    return seq


KEPT = {}


def rank_program(g, core, T, topo):
    rank = T.rank_of(core)
    if rank is None:
        return
    cfg = CFG
    dst = T.cores[(rank + 1) % len(T.cores)]
    rid, pid = topo.addr(dst)[:2]
    eng = topo.engines(core, dst); eng = eng[::len(eng) // cfg["engines"]]
    mask = sum(1 << e for e in eng)
    send = lambda out, in_, sem: g.remote_dma(out, in_, sem, T.sem.loc, pid, rid, mask)
    ops = build(g, T, send, cfg)
    if "seq" not in KEPT: KEPT["seq"] = arrange(ops, cfg)
    queue = {"v": g.vector, "a": g.scalar, "p": g.tensor, "g": g, "s": g.sync}
    known = {q: {} for q in queue}; total = {}; mark = {}; carry = {}
    for i in KEPT["seq"]:
        o = ops[i]; q = o["q"]
        if q is None:
            mark[i] = (o["sem"], o["inc"]); carry[i] = {}; total[o["sem"]] = o["inc"]
            continue
        need = {}
        for d in o["deps"]:
            s, val = mark[d]
            if val > need.get(s, (0, 0))[0]: need[s] = (val, d)
        for s, (val, d) in sorted(need.items(), key=lambda x: -x[1][1]):
            if known[q].get(s, 0) >= val: continue
            queue[q].wait_ge(T.sem[s], val)
            known[q][s] = val
            for s2, v2 in carry[d].items():
                if v2 > known[q].get(s2, 0): known[q][s2] = v2
        r = o["fn"]()
        if o["sem"] == "loc":
            total["loc"] = total.get("loc", 0) + len(eng)
            continue
        s = o["sem"] or COUNTER[q]
        r.then_inc(T.sem[s], o["inc"])
        total[s] = total.get(s, 0) + o["inc"]; mark[i] = (s, total[s]); carry[i] = dict(known[q])
    for s, val in total.items():
        if s == "loc": g.wait_ge(T.sem.loc, val)
        elif all(known[q].get(s, 0) < val for q in queue): g.sync.wait_ge(T.sem[s], val)
